import numpy as np
import ml_dtypes


def mxq(x, axis, fmt="e4m3"):
    dtype, down = {"e4m3": (ml_dtypes.float8_e4m3fn, 7), "e5m2": (ml_dtypes.float8_e5m2, 14)}[fmt]
    v = np.moveaxis(np.asarray(x, np.float32).astype(ml_dtypes.bfloat16).astype(np.float64), axis, -1)
    blocks = v.reshape(v.shape[:-1] + (-1, 32))
    amax = np.abs(blocks).max(-1, keepdims=True)
    byte = np.maximum(np.where(amax > 0, np.frexp(amax)[1] - 1 + 127, 0) - down, 1)
    scale = np.exp2(byte - 127.0)
    codes = (blocks / scale).astype(np.float32).astype(dtype).astype(np.float64)
    return np.moveaxis((codes * scale).reshape(v.shape), -1, axis)


WIDE = False


def mx_kscale(k):
    if not WIDE:
        return np.ones(k)
    levels = np.array([10, -10, 5, -5, 0])
    if k % 512:
        return np.exp2(np.random.permutation(np.resize(levels, k // 32))).repeat(32)
    a = np.empty((k // 512, 16))
    for p in range(k // 512):
        a[p, :8] = np.random.permutation(np.resize(levels, 8))
        for g in range(8):
            far = levels[np.abs(levels - a[p, g]) >= 10]
            a[p, g + 8] = far[np.random.randint(len(far))]
    return np.exp2(a.ravel()).repeat(32)


def f64(x):
    return np.asarray(x).astype(np.float64)


def striped(idx):
    return np.tile(idx.reshape(-1, 16).T, (8, 1)).astype(np.uint16)


def unstriped(offs):
    return offs[:16].T.reshape(-1).astype(np.int64)


def pack_weight(w):
    k, n = w.shape
    w = f64(np.asarray(w, np.float32).astype(ml_dtypes.bfloat16)).reshape(k // 32, 32, n)
    amax = np.abs(w).max(1)
    byte = np.clip(np.where(amax > 0, np.frexp(amax)[1] - 1 + 127 - 7, 1), 1, 254)
    scaled = (w * np.exp2(127.0 - byte)[:, None, :]).reshape(k, n).astype(np.float32)
    words = np.ascontiguousarray(scaled.reshape(k // 512, 128, 4, n).transpose(0, 1, 3, 2)).astype(ml_dtypes.float8_e4m3fn).view(np.uint8)
    return words, np.ascontiguousarray(byte.astype(np.uint8).reshape(k // 512, 16, n))


def unpack_weight(words, scales):
    g, p, n, _ = words.shape
    vals = np.ascontiguousarray(words).view(ml_dtypes.float8_e4m3fn).astype(np.float64) * np.repeat(np.exp2(scales.astype(np.float64) - 127.0), 8, axis=1)[..., None]
    return vals.transpose(0, 1, 3, 2).reshape(g * 512, n)


def relu(v):
    return np.maximum(v, 0.0)


K, T, S, N, U = 1024, 2048, 1024, 256, 2048


def setup_inputs():
    n = np.random.standard_normal
    s = mx_kscale(K)[:, None]
    packed_xT = pack_weight(n((K, T)) * s)
    return {
        "x_words": packed_xT[0],
        "x_scales": packed_xT[1],
        "w1": (n((K, N)) / np.sqrt(K) / s).astype(np.float32),
        "res": n((N, U)).astype(np.float32),
        "offs": striped(np.random.permutation(T)[:S]),
        "own": striped(np.random.randint(0, S, U)),
    }


def reference(x_words, x_scales, w1, res, offs, own):
    xq = unpack_weight(x_words, x_scales)[:, unstriped(offs)]
    y = relu(mxq(f64(w1), 0, "e4m3").T @ xq)
    return f64(res) + y[:, unstriped(own)]

@@ -1,0 +1,132 @@
+from contextlib import ExitStack
+
+import concourse.mybir as mybir
+
+K, T, S, N, U = 1024, 2048, 1024, 256, 2048
+FLOPS = 2 * K * N * S
+
+F32 = mybir.dt.float32
+BF16 = mybir.dt.bfloat16
+I32 = mybir.dt.int32
+U32 = mybir.dt.uint32
+U16 = mybir.dt.uint16
+U8 = mybir.dt.uint8
+FP8X4 = mybir.dt.float8_e4m3fn_x4
+RELU = mybir.ActivationFunctionType.Relu
+ADD = mybir.AluOpType.add
+
+P = 128
+PACK = 4
+PASSES = K // (P * PACK)
+BLOCKS = N // P
+LANES = 16
+PICK_PIECES = ((0, 512), (512, 768), (768, 1024))
+WIDE_PIECES = ((0, 512), (512, 1024))
+OUT_PIECES = (
+    ((0, 512), (512, 1024), (1024, 1536), (1536, 2048)),
+    ((0, 512), (512, 1024), (1024, 1536), (1536, 1856), (1856, 2048)),
+)
+RES_HALF = U // 2
+
+
+def tile_picked_unmerge_relu_p_kernel(tc, x_words, x_scales, w1, res, offs, own, out):
+    nc = tc.nc
+    with ExitStack() as ctx:
+        keep = ctx.enter_context(tc.tile_pool(name="keep", bufs=1))
+        psum = ctx.enter_context(tc.psum_pool(name="psum", bufs=1))
+
+        offs_sb = keep.tile([P, S // LANES], U16, name="offs_sb")
+        own_sb = keep.tile([P, U // LANES], U16, name="own_sb")
+        words = [keep.tile([P, T], I32, name="words%d" % z, align_bytes=64) for z in range(PASSES)]
+        scales = keep.tile([P, T], U8, name="scales", align_bytes=64)
+        w_raw = [[keep.tile([P, PACK, P], F32, name="w_raw%d%d" % (b, z), align_bytes=64) for z in range(PASSES)] for b in range(BLOCKS)]
+        w_bf = [keep.tile([P, PASSES, P, PACK], BF16, name="w_bf%d" % b, align_bytes=64) for b in range(BLOCKS)]
+        w_codes = [keep.tile([P, PASSES * P], U32, name="w_codes%d" % b, align_bytes=64) for b in range(BLOCKS)]
+        w_scales = [keep.tile([P, PASSES * P], U8, name="w_scales%d" % b, align_bytes=64) for b in range(BLOCKS)]
+        picked = [keep.tile([P, S], U32, name="picked%d" % z, align_bytes=64) for z in range(PASSES)]
+        picked_scales = keep.tile([P, S], U8, name="picked_scales", align_bytes=64)
+        res_sb = [[keep.tile([P, RES_HALF], F32, name="res%d%d" % (b, h), align_bytes=64) for h in range(2)] for b in range(BLOCKS)]
+        y = [keep.tile([P, S], F32, name="y%d" % b, align_bytes=64) for b in range(BLOCKS)]
+
+        def load_words(z):
+            nc.sync.dma_start(words[z][:], x_words[z].rearrange("p n t -> p (n t)").bitcast(I32))
+
+        def load_w(b):
+            for z in range(PASSES):
+                rows = w1[z * P * PACK : (z + 1) * P * PACK, b * P : (b + 1) * P]
+                nc.sync.dma_start(w_raw[b][z][:], rows.rearrange("(p j) m -> p j m", j=PACK))
+
+        def round_w(b):
+            for z in range(PASSES):
+                nc.scalar.copy(w_bf[b][:, z, :, :], w_raw[b][z][:].rearrange("p j m -> p m j"))
+
+        def quantize_w(b):
+            nc.vector.quantize_mx(
+                out=w_codes[b][:].bitcast(FP8X4),
+                scales=w_scales[b][:],
+                in_=w_bf[b][:].rearrange("p z m j -> p (z m j)"),
+            )
+
+        def pick_words(z, lo, hi):
+            window = words[z][:].bitcast(U32)
+            nc.vector.tensor_copy(picked[z][:, lo:hi], window.indirect(offs_sb[:, lo // LANES : hi // LANES]))
+
+        def product(acc, b, z, lo, hi):
+            nc.tensor.matmul_mx(
+                out=acc[:],
+                lhsT=w_codes[b][:, z * P : (z + 1) * P].bitcast(FP8X4),
+                lhsT_scale=w_scales[b][:, z * P : (z + 1) * P],
+                rhs=picked[z][:, lo:hi].bitcast(FP8X4),
+                rhs_scale=picked_scales[PACK * z : P, lo:hi],
+                start=(z == 0),
+                stop=(z == PASSES - 1),
+            )
+
+        def unmerge(b):
+            for lo, hi in OUT_PIECES[b]:
+                h = lo // RES_HALF
+                piece = keep.tile([P, hi - lo], F32, name="piece%d_%d" % (b, lo), align_bytes=64)
+                nc.vector.tensor_tensor(
+                    piece[:],
+                    y[b][:].indirect(own_sb[:, lo // LANES : hi // LANES]),
+                    res_sb[b][h][:, lo - h * RES_HALF : hi - h * RES_HALF],
+                    ADD,
+                )
+                nc.sync.dma_start(out[b * P : (b + 1) * P, lo:hi], piece[:])
+
+        nc.vector.memset(scales[:].bitcast(I32), 0)
+        nc.sync.dma_start(offs_sb[:], offs)
+        load_words(0)
+        for q in range(4):
+            nc.sync.dma_start(
+                scales[32 * q : 32 * q + PASSES * PACK, :].bitcast(I32),
+                x_scales[:, PACK * q : PACK * (q + 1), :].bitcast(I32),
+            )
+        load_w(0)
+        load_words(1)
+        nc.sync.dma_start(own_sb[:], own)
+        load_w(1)
+        for b in range(BLOCKS):
+            for h in range(2):
+                nc.sync.dma_start(res_sb[b][h][:], res[b * P : (b + 1) * P, h * RES_HALF : (h + 1) * RES_HALF])
+
+        pick_words(0, 0, S)
+        nc.vector.tensor_copy(picked_scales[:], scales[:].indirect(offs_sb[:]))
+        round_w(0)
+        quantize_w(0)
+        first = [psum.tile([P, hi - lo], F32, name="first%d" % lo) for lo, hi in PICK_PIECES]
+        for acc, (lo, hi) in zip(first, PICK_PIECES):
+            product(acc, 0, 0, lo, hi)
+        round_w(1)
+        for acc, (lo, hi) in zip(first, PICK_PIECES):
+            pick_words(1, lo, hi)
+            product(acc, 0, 1, lo, hi)
+            nc.scalar.activation(y[0][:, lo:hi], acc[:], RELU)
+        quantize_w(1)
+        for lo, hi in WIDE_PIECES:
+            acc = psum.tile([P, hi - lo], F32, name="second%d" % lo)
+            for z in range(PASSES):
+                product(acc, 1, z, lo, hi)
+            nc.scalar.activation(y[1][:, lo:hi], acc[:], RELU)
+        for b in range(BLOCKS):
+            unmerge(b)

@@ -13,6 +13,7 @@ U16 = mybir.dt.uint16
 U8 = mybir.dt.uint8
 FP8X4 = mybir.dt.float8_e4m3fn_x4
 RELU = mybir.ActivationFunctionType.Relu
+COPY = mybir.ActivationFunctionType.Copy
 ADD = mybir.AluOpType.add
 
 P = 128
@@ -21,12 +22,16 @@ PASSES = K // (P * PACK)
 BLOCKS = N // P
 LANES = 16
 PICK_PIECES = ((0, 512), (512, 768), (768, 1024))
-WIDE_PIECES = ((0, 512), (512, 1024))
+FIRST_GROUPS = ((0, 512), (512, 768), (768, 896), (896, 1024))
+SECOND_GROUPS = ((0, 512), (512, 768), (768, 1024))
 OUT_PIECES = (
-    ((0, 512), (512, 1024), (1024, 1536), (1536, 2048)),
-    ((0, 512), (512, 1024), (1024, 1536), (1536, 1856), (1856, 2048)),
+    ((0, 704), (704, 1376), (1376, 2048)),
+    ((0, 768), (768, 1536), (1536, 1920), (1920, 2048)),
 )
-RES_HALF = U // 2
+RES_PIECES = (
+    ((0, 704), (704, 2048)),
+    ((0, 768), (768, 2048)),
+)
 
 
 def tile_picked_unmerge_relu_p_kernel(tc, x_words, x_scales, w1, res, offs, own, out):
@@ -35,48 +40,55 @@ def tile_picked_unmerge_relu_p_kernel(tc, x_words, x_scales, w1, res, offs, own,
         keep = ctx.enter_context(tc.tile_pool(name="keep", bufs=1))
         psum = ctx.enter_context(tc.psum_pool(name="psum", bufs=1))
 
+        def sbuf(shape, dtype, name, tag=None):
+            return keep.tile(shape, dtype, name=name, tag=tag or name, align_bytes=64)
+
         offs_sb = keep.tile([P, S // LANES], U16, name="offs_sb")
         own_sb = keep.tile([P, U // LANES], U16, name="own_sb")
-        words = [keep.tile([P, T], I32, name="words%d" % z, align_bytes=64) for z in range(PASSES)]
-        scales = keep.tile([P, T], U8, name="scales", align_bytes=64)
-        w_raw = [[keep.tile([P, PACK, P], F32, name="w_raw%d%d" % (b, z), align_bytes=64) for z in range(PASSES)] for b in range(BLOCKS)]
-        w_bf = [keep.tile([P, PASSES, P, PACK], BF16, name="w_bf%d" % b, align_bytes=64) for b in range(BLOCKS)]
-        w_codes = [keep.tile([P, PASSES * P], U32, name="w_codes%d" % b, align_bytes=64) for b in range(BLOCKS)]
-        w_scales = [keep.tile([P, PASSES * P], U8, name="w_scales%d" % b, align_bytes=64) for b in range(BLOCKS)]
-        picked = [keep.tile([P, S], U32, name="picked%d" % z, align_bytes=64) for z in range(PASSES)]
-        picked_scales = keep.tile([P, S], U8, name="picked_scales", align_bytes=64)
-        res_sb = [[keep.tile([P, RES_HALF], F32, name="res%d%d" % (b, h), align_bytes=64) for h in range(2)] for b in range(BLOCKS)]
-        y = [keep.tile([P, S], F32, name="y%d" % b, align_bytes=64) for b in range(BLOCKS)]
+        words = [sbuf([P, T], I32, "words%d" % z) for z in range(PASSES)]
+        scales = sbuf([P, T], U8, "scales")
+        picked_scales = sbuf([P, S], U8, "picked_scales")
+        res_sb = [[sbuf([P, hi - lo], F32, "res%d_%d" % (b, lo)) for lo, hi in RES_PIECES[b]] for b in range(BLOCKS)]
+        w_raw, w_codes, w_scales, picked, y = {}, {}, {}, {}, {}
 
         def load_words(z):
             nc.sync.dma_start(words[z][:], x_words[z].rearrange("p n t -> p (n t)").bitcast(I32))
 
-        def load_w(b):
-            for z in range(PASSES):
-                rows = w1[z * P * PACK : (z + 1) * P * PACK, b * P : (b + 1) * P]
-                nc.sync.dma_start(w_raw[b][z][:], rows.rearrange("(p j) m -> p j m", j=PACK))
+        def load_w(b, z, dst):
+            w_raw[b, z] = dst
+            rows = w1[z * P * PACK : (z + 1) * P * PACK, b * P : (b + 1) * P]
+            nc.sync.dma_start(dst, rows.rearrange("(p j) m -> p j m", j=PACK))
 
-        def round_w(b):
-            for z in range(PASSES):
-                nc.scalar.copy(w_bf[b][:, z, :, :], w_raw[b][z][:].rearrange("p j m -> p m j"))
+        def round_w(b, passes):
+            rounded = sbuf([P, len(passes), P, PACK], BF16, "w_bf%d%d" % (b, passes[0]))
+            for n, z in enumerate(passes):
+                nc.scalar.activation(rounded[:, n, :, :], w_raw[b, z].rearrange("p j m -> p m j"), COPY)
+            return rounded
 
-        def quantize_w(b):
+        def quantize_w(b, passes, rounded, tag):
+            codes = sbuf([P, len(passes) * P], U32, "w_codes%d%d" % (b, passes[0]), tag)
+            plane = sbuf([P, len(passes) * P], U8, "w_scales%d%d" % (b, passes[0]))
             nc.vector.quantize_mx(
-                out=w_codes[b][:].bitcast(FP8X4),
-                scales=w_scales[b][:],
-                in_=w_bf[b][:].rearrange("p z m j -> p (z m j)"),
+                out=codes[:].bitcast(FP8X4),
+                scales=plane[:],
+                in_=rounded[:].rearrange("p z m j -> p (z m j)"),
             )
+            for n, z in enumerate(passes):
+                w_codes[b, z] = codes[:, n * P : (n + 1) * P]
+                w_scales[b, z] = plane[:, n * P : (n + 1) * P]
 
-        def pick_words(z, lo, hi):
+        def pick_words(z, lo, hi, tag=None):
             window = words[z][:].bitcast(U32)
-            nc.vector.tensor_copy(picked[z][:, lo:hi], window.indirect(offs_sb[:, lo // LANES : hi // LANES]))
+            picked[z, lo] = sbuf([P, hi - lo], U32, "picked%d_%d" % (z, lo), tag)
+            nc.vector.tensor_copy(picked[z, lo][:], window.indirect(offs_sb[:, lo // LANES : hi // LANES]))
 
         def product(acc, b, z, lo, hi):
+            base = max(start for zz, start in picked if zz == z and start <= lo)
             nc.tensor.matmul_mx(
                 out=acc[:],
-                lhsT=w_codes[b][:, z * P : (z + 1) * P].bitcast(FP8X4),
-                lhsT_scale=w_scales[b][:, z * P : (z + 1) * P],
-                rhs=picked[z][:, lo:hi].bitcast(FP8X4),
+                lhsT=w_codes[b, z].bitcast(FP8X4),
+                lhsT_scale=w_scales[b, z],
+                rhs=picked[z, base][:, lo - base : hi - base].bitcast(FP8X4),
                 rhs_scale=picked_scales[PACK * z : P, lo:hi],
                 start=(z == 0),
                 stop=(z == PASSES - 1),
@@ -84,46 +96,60 @@ def tile_picked_unmerge_relu_p_kernel(tc, x_words, x_scales, w1, res, offs, own,
 
         def unmerge(b):
             for lo, hi in OUT_PIECES[b]:
-                h = lo // RES_HALF
-                piece = keep.tile([P, hi - lo], F32, name="piece%d_%d" % (b, lo), align_bytes=64)
+                h = min(lo, 1)
+                base = RES_PIECES[b][h][0]
+                piece = sbuf([P, hi - lo], F32, "piece%d_%d" % (b, lo))
                 nc.vector.tensor_tensor(
                     piece[:],
                     y[b][:].indirect(own_sb[:, lo // LANES : hi // LANES]),
-                    res_sb[b][h][:, lo - h * RES_HALF : hi - h * RES_HALF],
+                    res_sb[b][h][:, lo - base : hi - base],
                     ADD,
                 )
                 nc.sync.dma_start(out[b * P : (b + 1) * P, lo:hi], piece[:])
 
+        raw00 = sbuf([P, PACK, P], F32, "raw00")
+        raw01 = sbuf([P, PACK, P], F32, "raw01")
+        raw1 = sbuf([P, PASSES, PACK, P], F32, "raw1")
+
         nc.vector.memset(scales[:].bitcast(I32), 0)
         nc.sync.dma_start(offs_sb[:], offs)
-        load_words(0)
+        nc.sync.dma_start(own_sb[:], own)
         for q in range(4):
             nc.sync.dma_start(
                 scales[32 * q : 32 * q + PASSES * PACK, :].bitcast(I32),
                 x_scales[:, PACK * q : PACK * (q + 1), :].bitcast(I32),
             )
-        load_w(0)
+        load_words(0)
+        load_w(0, 0, raw00[:])
         load_words(1)
-        nc.sync.dma_start(own_sb[:], own)
-        load_w(1)
+        load_w(0, 1, raw01[:])
+        load_w(1, 0, raw1[:, 0, :, :])
+        load_w(1, 1, raw1[:, 1, :, :])
         for b in range(BLOCKS):
-            for h in range(2):
-                nc.sync.dma_start(res_sb[b][h][:], res[b * P : (b + 1) * P, h * RES_HALF : (h + 1) * RES_HALF])
+            for tile, (lo, hi) in zip(res_sb[b], RES_PIECES[b]):
+                nc.sync.dma_start(tile[:], res[b * P : (b + 1) * P, lo:hi])
 
-        pick_words(0, 0, S)
         nc.vector.tensor_copy(picked_scales[:], scales[:].indirect(offs_sb[:]))
-        round_w(0)
-        quantize_w(0)
-        first = [psum.tile([P, hi - lo], F32, name="first%d" % lo) for lo, hi in PICK_PIECES]
-        for acc, (lo, hi) in zip(first, PICK_PIECES):
+        pick_words(0, 0, S)
+        quantize_w(0, (0,), round_w(0, (0,)), "words0")
+        first = [psum.tile([P, hi - lo], F32, name="first%d" % lo) for lo, hi in FIRST_GROUPS]
+        for acc, (lo, hi) in zip(first, FIRST_GROUPS):
             product(acc, 0, 0, lo, hi)
-        round_w(1)
-        for acc, (lo, hi) in zip(first, PICK_PIECES):
-            pick_words(1, lo, hi)
+        pick_words(1, 0, 512)
+        quantize_w(0, (1,), round_w(0, (1,)), None)
+        rounded1 = round_w(1, (0, 1))
+        pick_words(1, 512, 768, "w_bf01")
+        pick_words(1, 768, 1024, "raw01")
+        quantize_w(1, (0, 1), rounded1, "words1")
+        y[0] = sbuf([P, S], F32, "y0", "raw1")
+        y[1] = sbuf([P, S], F32, "y1")
+        for acc, (lo, hi) in zip(first, FIRST_GROUPS):
             product(acc, 0, 1, lo, hi)
-            nc.scalar.activation(y[0][:, lo:hi], acc[:], RELU)
-        quantize_w(1)
-        for lo, hi in WIDE_PIECES:
+            if hi < S:
+                nc.scalar.activation(y[0][:, lo:hi], acc[:], RELU)
+            else:
+                nc.vector.tensor_scalar_max(y[0][:, lo:hi], acc[:], 0.0)
+        for lo, hi in SECOND_GROUPS:
             acc = psum.tile([P, hi - lo], F32, name="second%d" % lo)
             for z in range(PASSES):
                 product(acc, 1, z, lo, hi)

@@ -62,7 +62,11 @@ def tile_picked_unmerge_relu_p_kernel(tc, x_words, x_scales, w1, res, offs, own,
         def round_w(b, passes):
             rounded = sbuf([P, len(passes), P, PACK], BF16, "w_bf%d%d" % (b, passes[0]))
             for n, z in enumerate(passes):
-                nc.scalar.activation(rounded[:, n, :, :], w_raw[b, z].rearrange("p j m -> p m j"), COPY)
+                nc.scalar.activation(
+                    rounded[:, n, :, :].rearrange("p (c i) j -> p c j i", i=4),
+                    w_raw[b, z].rearrange("p j (c i) -> p c j i", i=4),
+                    COPY,
+                )
             return rounded
 
         def quantize_w(b, passes, rounded, tag):
@@ -145,7 +149,7 @@ def tile_picked_unmerge_relu_p_kernel(tc, x_words, x_scales, w1, res, offs, own,
         y[1] = sbuf([P, S], F32, "y1")
         for acc, (lo, hi) in zip(first, FIRST_GROUPS):
             product(acc, 0, 1, lo, hi)
-            if hi < S:
+            if lo != 768:
                 nc.scalar.activation(y[0][:, lo:hi], acc[:], RELU)
             else:
                 nc.vector.tensor_scalar_max(y[0][:, lo:hi], acc[:], 0.0)

@@ -19,18 +19,16 @@ ADD = mybir.AluOpType.add
 P = 128
 PACK = 4
 PASSES = K // (P * PACK)
-BLOCKS = N // P
-LANES = 16
-PICK_PIECES = ((0, 512), (512, 768), (768, 1024))
-FIRST_GROUPS = ((0, 512), (512, 768), (768, 896), (896, 1024))
-SECOND_GROUPS = ((0, 512), (512, 768), (768, 1024))
-OUT_PIECES = (
+QUADRANT = 32
+ROW_BLOCKS = N // P
+ENTRIES_PER_COLUMN = 16
+LINE = 4
+
+PICK_RANGES = ((0, 512), (512, 768), (768, 1024))
+BANK_RANGES = ((0, 512), (512, 1024))
+OUT_RANGES = (
     ((0, 704), (704, 1376), (1376, 2048)),
     ((0, 768), (768, 1536), (1536, 1920), (1920, 2048)),
-)
-RES_PIECES = (
-    ((0, 704), (704, 2048)),
-    ((0, 768), (768, 2048)),
 )
 
 
@@ -40,123 +38,133 @@ def tile_picked_unmerge_relu_p_kernel(tc, x_words, x_scales, w1, res, offs, own,
         keep = ctx.enter_context(tc.tile_pool(name="keep", bufs=1))
         psum = ctx.enter_context(tc.psum_pool(name="psum", bufs=1))
 
-        def sbuf(shape, dtype, name, tag=None):
-            return keep.tile(shape, dtype, name=name, tag=tag or name, align_bytes=64)
+        def sbuf(shape, dtype, name, after=None):
+            return keep.tile(shape, dtype, name=name, tag=after or name, align_bytes=64)
 
-        offs_sb = keep.tile([P, S // LANES], U16, name="offs_sb")
-        own_sb = keep.tile([P, U // LANES], U16, name="own_sb")
+        def entries(list_tile, lo, hi):
+            return list_tile[:, lo // ENTRIES_PER_COLUMN : hi // ENTRIES_PER_COLUMN]
+
+        offs_sb = keep.tile([P, S // ENTRIES_PER_COLUMN], U16, name="offs_sb")
+        own_sb = keep.tile([P, U // ENTRIES_PER_COLUMN], U16, name="own_sb")
         words = [sbuf([P, T], I32, "words%d" % z) for z in range(PASSES)]
         scales = sbuf([P, T], U8, "scales")
         picked_scales = sbuf([P, S], U8, "picked_scales")
-        res_sb = [[sbuf([P, hi - lo], F32, "res%d_%d" % (b, lo)) for lo, hi in RES_PIECES[b]] for b in range(BLOCKS)]
-        w_raw, w_codes, w_scales, picked, y = {}, {}, {}, {}, {}
+        res_ranges = [(ranges[0], (ranges[0][1], U)) for ranges in OUT_RANGES]
+        res_sb = [[sbuf([P, hi - lo], F32, "res%d_%d" % (b, lo)) for lo, hi in res_ranges[b]] for b in range(ROW_BLOCKS)]
+        raw00 = sbuf([P, PACK, P], F32, "raw00")
+        raw01 = sbuf([P, PACK, P], F32, "raw01")
+        raw1 = sbuf([P, PASSES, PACK, P], F32, "raw1")
+        w_raw = {(0, 0): raw00[:], (0, 1): raw01[:], (1, 0): raw1[:, 0, :, :], (1, 1): raw1[:, 1, :, :]}
+        w_codes, w_scales = {}, {}
+        picked_words = {}
 
         def load_words(z):
             nc.sync.dma_start(words[z][:], x_words[z].rearrange("p n t -> p (n t)").bitcast(I32))
 
-        def load_w(b, z, dst):
-            w_raw[b, z] = dst
+        def load_w(b, z):
             rows = w1[z * P * PACK : (z + 1) * P * PACK, b * P : (b + 1) * P]
-            nc.sync.dma_start(dst, rows.rearrange("(p j) m -> p j m", j=PACK))
+            nc.sync.dma_start(w_raw[b, z], rows.rearrange("(p t) m -> p t m", t=PACK))
 
         def round_w(b, passes):
-            rounded = sbuf([P, len(passes), P, PACK], BF16, "w_bf%d%d" % (b, passes[0]))
+            rounded = sbuf([P, len(passes), P, PACK], BF16, "rounded%d%d" % (b, passes[0]))
             for n, z in enumerate(passes):
                 nc.scalar.activation(
-                    rounded[:, n, :, :].rearrange("p (c i) j -> p c j i", i=4),
-                    w_raw[b, z].rearrange("p j (c i) -> p c j i", i=4),
+                    rounded[:, n, :, :].rearrange("p (c i) t -> p c t i", i=LINE),
+                    w_raw[b, z].rearrange("p t (c i) -> p c t i", i=LINE),
                     COPY,
                 )
             return rounded
 
-        def quantize_w(b, passes, rounded, tag):
-            codes = sbuf([P, len(passes) * P], U32, "w_codes%d%d" % (b, passes[0]), tag)
-            plane = sbuf([P, len(passes) * P], U8, "w_scales%d%d" % (b, passes[0]))
+        def quantize_w(b, passes, rounded):
+            codes = sbuf([P, len(passes) * P], U32, "w_codes%d%d" % (b, passes[0]))
+            scale_bytes = sbuf([P, len(passes) * P], U8, "w_scales%d%d" % (b, passes[0]))
             nc.vector.quantize_mx(
                 out=codes[:].bitcast(FP8X4),
-                scales=plane[:],
-                in_=rounded[:].rearrange("p z m j -> p (z m j)"),
+                scales=scale_bytes[:],
+                in_=rounded[:].rearrange("p n m t -> p (n m t)"),
             )
             for n, z in enumerate(passes):
                 w_codes[b, z] = codes[:, n * P : (n + 1) * P]
-                w_scales[b, z] = plane[:, n * P : (n + 1) * P]
+                w_scales[b, z] = scale_bytes[:, n * P : (n + 1) * P]
 
-        def pick_words(z, lo, hi, tag=None):
-            window = words[z][:].bitcast(U32)
-            picked[z, lo] = sbuf([P, hi - lo], U32, "picked%d_%d" % (z, lo), tag)
-            nc.vector.tensor_copy(picked[z, lo][:], window.indirect(offs_sb[:, lo // LANES : hi // LANES]))
+        def pick_words(z, ranges, after=None):
+            first = ranges[0][0]
+            dst = sbuf([P, ranges[-1][1] - first], U32, "picked_words%d_%d" % (z, first), after)
+            picked_words[z, first] = dst
+            for lo, hi in ranges:
+                nc.vector.tensor_copy(dst[:, lo - first : hi - first], words[z][:].bitcast(U32).indirect(entries(offs_sb, lo, hi)))
 
         def product(acc, b, z, lo, hi):
-            base = max(start for zz, start in picked if zz == z and start <= lo)
+            first = max(start for pass_of_tile, start in picked_words if pass_of_tile == z and start <= lo)
             nc.tensor.matmul_mx(
                 out=acc[:],
                 lhsT=w_codes[b, z].bitcast(FP8X4),
                 lhsT_scale=w_scales[b, z],
-                rhs=picked[z, base][:, lo - base : hi - base].bitcast(FP8X4),
+                rhs=picked_words[z, first][:, lo - first : hi - first].bitcast(FP8X4),
                 rhs_scale=picked_scales[PACK * z : P, lo:hi],
                 start=(z == 0),
                 stop=(z == PASSES - 1),
             )
 
-        def unmerge(b):
-            for lo, hi in OUT_PIECES[b]:
-                h = min(lo, 1)
-                base = RES_PIECES[b][h][0]
-                piece = sbuf([P, hi - lo], F32, "piece%d_%d" % (b, lo))
+        def unmerge(b, y):
+            for n, (lo, hi) in enumerate(OUT_RANGES[b]):
+                part = min(n, 1)
+                first = res_ranges[b][part][0]
+                sums = sbuf([P, hi - lo], F32, "sums%d_%d" % (b, lo))
                 nc.vector.tensor_tensor(
-                    piece[:],
-                    y[b][:].indirect(own_sb[:, lo // LANES : hi // LANES]),
-                    res_sb[b][h][:, lo - base : hi - base],
+                    sums[:],
+                    y[:].indirect(entries(own_sb, lo, hi)),
+                    res_sb[b][part][:, lo - first : hi - first],
                     ADD,
                 )
-                nc.sync.dma_start(out[b * P : (b + 1) * P, lo:hi], piece[:])
-
-        raw00 = sbuf([P, PACK, P], F32, "raw00")
-        raw01 = sbuf([P, PACK, P], F32, "raw01")
-        raw1 = sbuf([P, PASSES, PACK, P], F32, "raw1")
+                nc.sync.dma_start(out[b * P : (b + 1) * P, lo:hi], sums[:])
 
         nc.vector.memset(scales[:].bitcast(I32), 0)
+
         nc.sync.dma_start(offs_sb[:], offs)
         nc.sync.dma_start(own_sb[:], own)
-        for q in range(4):
+        for q in range(P // QUADRANT):
             nc.sync.dma_start(
-                scales[32 * q : 32 * q + PASSES * PACK, :].bitcast(I32),
+                scales[QUADRANT * q : QUADRANT * q + PASSES * PACK, :].bitcast(I32),
                 x_scales[:, PACK * q : PACK * (q + 1), :].bitcast(I32),
             )
         load_words(0)
-        load_w(0, 0, raw00[:])
+        load_w(0, 0)
         load_words(1)
-        load_w(0, 1, raw01[:])
-        load_w(1, 0, raw1[:, 0, :, :])
-        load_w(1, 1, raw1[:, 1, :, :])
-        for b in range(BLOCKS):
-            for tile, (lo, hi) in zip(res_sb[b], RES_PIECES[b]):
-                nc.sync.dma_start(tile[:], res[b * P : (b + 1) * P, lo:hi])
+        load_w(0, 1)
+        load_w(1, 0)
+        load_w(1, 1)
+        for b in range(ROW_BLOCKS):
+            for dst, (lo, hi) in zip(res_sb[b], res_ranges[b]):
+                nc.sync.dma_start(dst[:], res[b * P : (b + 1) * P, lo:hi])
 
         nc.vector.tensor_copy(picked_scales[:], scales[:].indirect(offs_sb[:]))
-        pick_words(0, 0, S)
-        quantize_w(0, (0,), round_w(0, (0,)), "words0")
-        first = [psum.tile([P, hi - lo], F32, name="first%d" % lo) for lo, hi in FIRST_GROUPS]
-        for acc, (lo, hi) in zip(first, FIRST_GROUPS):
+        pick_words(0, ((0, S),))
+        quantize_w(0, (0,), round_w(0, (0,)))
+        accs = [psum.tile([P, hi - lo], F32, name="acc0_%d" % lo) for lo, hi in PICK_RANGES]
+        for acc, (lo, hi) in zip(accs, PICK_RANGES):
             product(acc, 0, 0, lo, hi)
-        pick_words(1, 0, 512)
-        quantize_w(0, (1,), round_w(0, (1,)), None)
+
+        pick_words(1, PICK_RANGES[:1])
+        quantize_w(0, (1,), round_w(0, (1,)))
         rounded1 = round_w(1, (0, 1))
-        pick_words(1, 512, 768, "w_bf01")
-        pick_words(1, 768, 1024, "raw01")
-        quantize_w(1, (0, 1), rounded1, "words1")
-        y[0] = sbuf([P, S], F32, "y0", "raw1")
-        y[1] = sbuf([P, S], F32, "y1")
-        for acc, (lo, hi) in zip(first, FIRST_GROUPS):
+        pick_words(1, PICK_RANGES[1:], after="raw01")
+        quantize_w(1, (0, 1), rounded1)
+
+        y0 = sbuf([P, S], F32, "y0", after="raw1")
+        y1 = sbuf([P, S], F32, "y1")
+        for acc, (lo, hi) in zip(accs, PICK_RANGES):
             product(acc, 0, 1, lo, hi)
-            if lo != 768:
-                nc.scalar.activation(y[0][:, lo:hi], acc[:], RELU)
+            if hi < S:
+                nc.scalar.activation(y0[:, lo:hi], acc[:], RELU)
             else:
-                nc.vector.tensor_scalar_max(y[0][:, lo:hi], acc[:], 0.0)
-        for lo, hi in SECOND_GROUPS:
-            acc = psum.tile([P, hi - lo], F32, name="second%d" % lo)
+                nc.vector.tensor_scalar_max(y0[:, lo:hi], acc[:], 0.0)
+
+        for lo, hi in BANK_RANGES:
+            acc = psum.tile([P, hi - lo], F32, name="acc1_%d" % lo)
             for z in range(PASSES):
                 product(acc, 1, z, lo, hi)
-            nc.scalar.activation(y[1][:, lo:hi], acc[:], RELU)
-        for b in range(BLOCKS):
-            unmerge(b)
+            nc.scalar.activation(y1[:, lo:hi], acc[:], RELU)
+
+        unmerge(0, y0)
+        unmerge(1, y1)

@@ -24,21 +24,26 @@ ROW_BLOCKS = N // P
 ENTRIES_PER_COLUMN = 16
 LINE = 4
 
-PICK_RANGES = ((0, 512), (512, 768), (768, 1024))
-BANK_RANGES = ((0, 512), (512, 1024))
+LAST_PICK = 512
+CHUNK = 256
+BANK = 512
 OUT_RANGES = (
-    ((0, 704), (704, 1376), (1376, 2048)),
+    ((0, 512), (512, 1280), (1280, 2048)),
     ((0, 768), (768, 1536), (1536, 1920), (1920, 2048)),
 )
+AT_WORDS0, AT_RAW11, AT_RES0, AT_WORDS1, AT_RES1 = 0, 0, 2048, 10240, 10240
 
 
 def tile_picked_unmerge_relu_p_kernel(tc, x_words, x_scales, w1, res, offs, own, out):
     nc = tc.nc
     with ExitStack() as ctx:
         keep = ctx.enter_context(tc.tile_pool(name="keep", bufs=1))
+        laid = ctx.enter_context(tc.tile_pool(name="laid", bufs=1))
         psum = ctx.enter_context(tc.psum_pool(name="psum", bufs=1))
 
-        def sbuf(shape, dtype, name, after=None):
+        def sbuf(shape, dtype, name, after=None, at=None):
+            if at is not None:
+                return laid.tile(shape, dtype, name=name, tag=name, align_bytes=64, offset=at)
             return keep.tile(shape, dtype, name=name, tag=after or name, align_bytes=64)
 
         def entries(list_tile, lo, hi):
@@ -46,37 +51,36 @@ def tile_picked_unmerge_relu_p_kernel(tc, x_words, x_scales, w1, res, offs, own,
 
         offs_sb = keep.tile([P, S // ENTRIES_PER_COLUMN], U16, name="offs_sb")
         own_sb = keep.tile([P, U // ENTRIES_PER_COLUMN], U16, name="own_sb")
-        words = [sbuf([P, T], I32, "words%d" % z) for z in range(PASSES)]
+        words = [sbuf([P, T], I32, "words0", at=AT_WORDS0), sbuf([P, T], I32, "words1", at=AT_WORDS1)]
         scales = sbuf([P, T], U8, "scales")
         picked_scales = sbuf([P, S], U8, "picked_scales")
-        res_ranges = [(ranges[0], (ranges[0][1], U)) for ranges in OUT_RANGES]
-        res_sb = [[sbuf([P, hi - lo], F32, "res%d_%d" % (b, lo)) for lo, hi in res_ranges[b]] for b in range(ROW_BLOCKS)]
-        raw00 = sbuf([P, PACK, P], F32, "raw00")
-        raw01 = sbuf([P, PACK, P], F32, "raw01")
-        raw1 = sbuf([P, PASSES, PACK, P], F32, "raw1")
-        w_raw = {(0, 0): raw00[:], (0, 1): raw01[:], (1, 0): raw1[:, 0, :, :], (1, 1): raw1[:, 1, :, :]}
-        w_codes, w_scales = {}, {}
-        picked_words = {}
+        placed_scales = sbuf([P, PASSES * S], U8, "placed_scales")
+        w_raw, w_codes, w_scales, picked_words, res_sb = {}, {}, {}, {}, {}
 
         def load_words(z):
             nc.sync.dma_start(words[z][:], x_words[z].rearrange("p n t -> p (n t)").bitcast(I32))
 
-        def load_w(b, z):
+        def load_w(b, z, after=None, at=None):
+            w_raw[b, z] = sbuf([P, PACK, P], F32, "raw%d%d" % (b, z), after, at)
             rows = w1[z * P * PACK : (z + 1) * P * PACK, b * P : (b + 1) * P]
-            nc.sync.dma_start(w_raw[b, z], rows.rearrange("(p t) m -> p t m", t=PACK))
+            nc.sync.dma_start(w_raw[b, z][:], rows.rearrange("(p t) m -> p t m", t=PACK))
 
-        def round_w(b, passes):
-            rounded = sbuf([P, len(passes), P, PACK], BF16, "rounded%d%d" % (b, passes[0]))
+        def load_res(b, lo, hi, after=None, at=None):
+            res_sb[b, lo] = sbuf([P, hi - lo], F32, "res%d_%d" % (b, lo), after, at)
+            nc.sync.dma_start(res_sb[b, lo][:], res[b * P : (b + 1) * P, lo:hi])
+
+        def round_w(b, passes, after=None):
+            rounded = sbuf([P, len(passes), P, PACK], BF16, "rounded%d%d" % (b, passes[0]), after)
             for n, z in enumerate(passes):
                 nc.scalar.activation(
                     rounded[:, n, :, :].rearrange("p (c i) t -> p c t i", i=LINE),
-                    w_raw[b, z].rearrange("p t (c i) -> p c t i", i=LINE),
+                    w_raw[b, z][:].rearrange("p t (c i) -> p c t i", i=LINE),
                     COPY,
                 )
             return rounded
 
-        def quantize_w(b, passes, rounded):
-            codes = sbuf([P, len(passes) * P], U32, "w_codes%d%d" % (b, passes[0]))
+        def quantize_w(b, passes, rounded, after=None):
+            codes = sbuf([P, len(passes) * P], U32, "w_codes%d%d" % (b, passes[0]), after)
             scale_bytes = sbuf([P, len(passes) * P], U8, "w_scales%d%d" % (b, passes[0]))
             nc.vector.quantize_mx(
                 out=codes[:].bitcast(FP8X4),
@@ -87,84 +91,81 @@ def tile_picked_unmerge_relu_p_kernel(tc, x_words, x_scales, w1, res, offs, own,
                 w_codes[b, z] = codes[:, n * P : (n + 1) * P]
                 w_scales[b, z] = scale_bytes[:, n * P : (n + 1) * P]
 
-        def pick_words(z, ranges, after=None):
-            first = ranges[0][0]
-            dst = sbuf([P, ranges[-1][1] - first], U32, "picked_words%d_%d" % (z, first), after)
-            picked_words[z, first] = dst
-            for lo, hi in ranges:
-                nc.vector.tensor_copy(dst[:, lo - first : hi - first], words[z][:].bitcast(U32).indirect(entries(offs_sb, lo, hi)))
+        def pick_words(z, lo, hi, after=None):
+            dst = sbuf([P, hi - lo], U32, "picked_words%d_%d" % (z, lo), after)
+            picked_words[z, lo] = dst
+            nc.vector.tensor_copy(dst[:], words[z][:].bitcast(U32).indirect(entries(offs_sb, lo, hi)))
 
         def product(acc, b, z, lo, hi):
             first = max(start for pass_of_tile, start in picked_words if pass_of_tile == z and start <= lo)
             nc.tensor.matmul_mx(
-                out=acc[:],
+                out=acc,
                 lhsT=w_codes[b, z].bitcast(FP8X4),
                 lhsT_scale=w_scales[b, z],
                 rhs=picked_words[z, first][:, lo - first : hi - first].bitcast(FP8X4),
-                rhs_scale=picked_scales[PACK * z : P, lo:hi],
+                rhs_scale=placed_scales[:, z * S + lo : z * S + hi],
                 start=(z == 0),
                 stop=(z == PASSES - 1),
             )
 
-        def unmerge(b, y):
-            for n, (lo, hi) in enumerate(OUT_RANGES[b]):
-                part = min(n, 1)
-                first = res_ranges[b][part][0]
-                sums = sbuf([P, hi - lo], F32, "sums%d_%d" % (b, lo))
-                nc.vector.tensor_tensor(
-                    sums[:],
-                    y[:].indirect(entries(own_sb, lo, hi)),
-                    res_sb[b][part][:, lo - first : hi - first],
-                    ADD,
-                )
-                nc.sync.dma_start(out[b * P : (b + 1) * P, lo:hi], sums[:])
+        def unmerge(b, y, n, at=None):
+            lo, hi = OUT_RANGES[b][n]
+            first = max(start for block, start in res_sb if block == b and start <= lo)
+            sums = sbuf([P, hi - lo], F32, "sums%d_%d" % (b, lo), at=at)
+            nc.vector.tensor_tensor(
+                sums[:],
+                y[:].indirect(entries(own_sb, lo, hi)),
+                res_sb[b, first][:, lo - first : hi - first],
+                ADD,
+            )
+            nc.sync.dma_start(out[b * P : (b + 1) * P, lo:hi], sums[:])
 
         nc.vector.memset(scales[:].bitcast(I32), 0)
+        nc.vector.memset(placed_scales[:].bitcast(I32), 0)
 
         nc.sync.dma_start(offs_sb[:], offs)
         nc.sync.dma_start(own_sb[:], own)
-        for q in range(P // QUADRANT):
-            nc.sync.dma_start(
-                scales[QUADRANT * q : QUADRANT * q + PASSES * PACK, :].bitcast(I32),
-                x_scales[:, PACK * q : PACK * (q + 1), :].bitcast(I32),
-            )
+        nc.sync.dma_start(scales[0:P:PACK, :].bitcast(I32), x_scales.rearrange("z r n -> r z n").bitcast(I32))
         load_words(0)
-        load_w(0, 0)
         load_words(1)
+        load_w(0, 0)
         load_w(0, 1)
-        load_w(1, 0)
-        load_w(1, 1)
-        for b in range(ROW_BLOCKS):
-            for dst, (lo, hi) in zip(res_sb[b], res_ranges[b]):
-                nc.sync.dma_start(dst[:], res[b * P : (b + 1) * P, lo:hi])
 
         nc.vector.tensor_copy(picked_scales[:], scales[:].indirect(offs_sb[:]))
-        pick_words(0, ((0, S),))
+        for q in range(P // QUADRANT):
+            nc.sync.dma_start(
+                placed_scales[QUADRANT * q : QUADRANT * q + PACK, :].bitcast(I32),
+                picked_scales[QUADRANT * q : QUADRANT * (q + 1) : PACK, :].bitcast(I32),
+            )
+        load_w(1, 0, after="scales")
+
+        pick_words(0, 0, S)
+        load_w(1, 1, at=AT_RAW11)
+        for lo, hi in OUT_RANGES[0]:
+            load_res(0, lo, hi, at=AT_RES0 + 4 * lo)
+
+        pick_words(1, 0, LAST_PICK)
         quantize_w(0, (0,), round_w(0, (0,)))
-        accs = [psum.tile([P, hi - lo], F32, name="acc0_%d" % lo) for lo, hi in PICK_RANGES]
-        for acc, (lo, hi) in zip(accs, PICK_RANGES):
-            product(acc, 0, 0, lo, hi)
-
-        pick_words(1, PICK_RANGES[:1])
+        pick_words(1, LAST_PICK, S, after="raw00")
+        load_res(1, 0, OUT_RANGES[1][0][1], at=AT_RES1)
+        load_res(1, OUT_RANGES[1][0][1], U, at=AT_RES1 + 4 * OUT_RANGES[1][0][1])
         quantize_w(0, (1,), round_w(0, (1,)))
-        rounded1 = round_w(1, (0, 1))
-        pick_words(1, PICK_RANGES[1:], after="raw01")
-        quantize_w(1, (0, 1), rounded1)
 
-        y0 = sbuf([P, S], F32, "y0", after="raw1")
+        y0 = sbuf([P, S], F32, "y0")
         y1 = sbuf([P, S], F32, "y1")
-        for acc, (lo, hi) in zip(accs, PICK_RANGES):
-            product(acc, 0, 1, lo, hi)
-            if hi < S:
-                nc.scalar.activation(y0[:, lo:hi], acc[:], RELU)
-            else:
-                nc.vector.tensor_scalar_max(y0[:, lo:hi], acc[:], 0.0)
+        accs = [psum.tile([P, CHUNK], F32, name="acc0_%d" % lo) for lo in range(0, S, CHUNK)]
+        for c, acc in enumerate(accs):
+            product(acc[:], 0, 0, c * CHUNK, (c + 1) * CHUNK)
+        for c, acc in enumerate(accs):
+            product(acc[:], 0, 1, c * CHUNK, (c + 1) * CHUNK)
+            nc.vector.tensor_scalar_max(y0[:, c * CHUNK : (c + 1) * CHUNK], acc[:], 0.0)
 
-        for lo, hi in BANK_RANGES:
-            acc = psum.tile([P, hi - lo], F32, name="acc1_%d" % lo)
+        quantize_w(1, (0, 1), round_w(1, (0, 1)), after="w_codes01")
+        for lo in range(0, S, BANK):
+            acc = psum.tile([P, BANK], F32, name="acc1_%d" % lo)
             for z in range(PASSES):
-                product(acc, 1, z, lo, hi)
-            nc.scalar.activation(y1[:, lo:hi], acc[:], RELU)
-
-        unmerge(0, y0)
-        unmerge(1, y1)
+                product(acc[:], 1, z, lo, lo + BANK)
+            nc.scalar.activation(y1[:, lo : lo + BANK], acc[:], RELU)
+        for b, y in enumerate((y0, y1)):
+            for n in range(len(OUT_RANGES[b])):
+                unmerge(b, y, n)

@@ -24,8 +24,9 @@ ROW_BLOCKS = N // P
 ENTRIES_PER_COLUMN = 16
 LINE = 4
 
-LAST_PICK = 512
-CHUNK = 256
+PICK_RANGES = ((0, 512), (512, 768), (768, 1024))
+CHUNKS = ((0, 256), (256, 512), (512, 768), (768, 896), (896, 1024))
+SCALE_ROWS = 32
 BANK = 512
 OUT_RANGES = (
     ((0, 512), (512, 1280), (1280, 2048)),
@@ -120,22 +121,23 @@ def tile_picked_unmerge_relu_p_kernel(tc, x_words, x_scales, w1, res, offs, own,
             )
             nc.sync.dma_start(out[b * P : (b + 1) * P, lo:hi], sums[:])
 
-        nc.vector.memset(scales[:].bitcast(I32), 0)
+        nc.vector.memset(scales[: P - SCALE_ROWS, :].bitcast(I32), 0)
         nc.vector.memset(placed_scales[:].bitcast(I32), 0)
 
+        nc.sync.dma_start(scales[P - SCALE_ROWS :, :].bitcast(I32), x_scales.rearrange("z r n -> r z n").bitcast(I32))
         nc.sync.dma_start(offs_sb[:], offs)
-        nc.sync.dma_start(own_sb[:], own)
-        nc.sync.dma_start(scales[0:P:PACK, :].bitcast(I32), x_scales.rearrange("z r n -> r z n").bitcast(I32))
         load_words(0)
+        nc.sync.dma_start(own_sb[:], own)
         load_words(1)
         load_w(0, 0)
         load_w(0, 1)
 
         nc.vector.tensor_copy(picked_scales[:], scales[:].indirect(offs_sb[:]))
-        for q in range(P // QUADRANT):
+        for q in (0, 2, 1, 3):
+            row = P - SCALE_ROWS + PASSES * PACK * q
             nc.sync.dma_start(
                 placed_scales[QUADRANT * q : QUADRANT * q + PACK, :].bitcast(I32),
-                picked_scales[QUADRANT * q : QUADRANT * (q + 1) : PACK, :].bitcast(I32),
+                picked_scales[row : row + PASSES * PACK, :].bitcast(I32),
             )
         load_w(1, 0, after="scales")
 
@@ -144,28 +146,29 @@ def tile_picked_unmerge_relu_p_kernel(tc, x_words, x_scales, w1, res, offs, own,
         for lo, hi in OUT_RANGES[0]:
             load_res(0, lo, hi, at=AT_RES0 + 4 * lo)
 
-        pick_words(1, 0, LAST_PICK)
+        pick_words(1, *PICK_RANGES[0])
         quantize_w(0, (0,), round_w(0, (0,)))
-        pick_words(1, LAST_PICK, S, after="raw00")
+        pick_words(1, *PICK_RANGES[1], after="raw00")
+        quantize_w(0, (1,), round_w(0, (1,)))
+        pick_words(1, *PICK_RANGES[2], after="raw01")
         load_res(1, 0, OUT_RANGES[1][0][1], at=AT_RES1)
         load_res(1, OUT_RANGES[1][0][1], U, at=AT_RES1 + 4 * OUT_RANGES[1][0][1])
-        quantize_w(0, (1,), round_w(0, (1,)))
 
         y0 = sbuf([P, S], F32, "y0")
         y1 = sbuf([P, S], F32, "y1")
-        accs = [psum.tile([P, CHUNK], F32, name="acc0_%d" % lo) for lo in range(0, S, CHUNK)]
-        for c, acc in enumerate(accs):
-            product(acc[:], 0, 0, c * CHUNK, (c + 1) * CHUNK)
-        for c, acc in enumerate(accs):
-            product(acc[:], 0, 1, c * CHUNK, (c + 1) * CHUNK)
-            nc.vector.tensor_scalar_max(y0[:, c * CHUNK : (c + 1) * CHUNK], acc[:], 0.0)
+        accs = [psum.tile([P, hi - lo], F32, name="acc0_%d" % lo) for lo, hi in CHUNKS]
+        for acc, (lo, hi) in zip(accs, CHUNKS):
+            product(acc[:], 0, 0, lo, hi)
+        for acc, (lo, hi) in zip(accs, CHUNKS):
+            product(acc[:], 0, 1, lo, hi)
+            nc.vector.tensor_scalar_max(y0[:, lo:hi], acc[:], 0.0)
 
         quantize_w(1, (0, 1), round_w(1, (0, 1)), after="w_codes01")
-        for lo in range(0, S, BANK):
-            acc = psum.tile([P, BANK], F32, name="acc1_%d" % lo)
+        for lo, hi in PICK_RANGES:
+            acc = psum.tile([P, hi - lo], F32, name="acc1_%d" % lo)
             for z in range(PASSES):
-                product(acc[:], 1, z, lo, lo + BANK)
-            nc.scalar.activation(y1[:, lo : lo + BANK], acc[:], RELU)
+                product(acc[:], 1, z, lo, hi)
+            nc.scalar.activation(y1[:, lo:hi], acc[:], RELU)
         for b, y in enumerate((y0, y1)):
             for n in range(len(OUT_RANGES[b])):
                 unmerge(b, y, n)

@@ -29,10 +29,10 @@ CHUNKS = ((0, 256), (256, 512), (512, 768), (768, 896), (896, 1024))
 SCALE_ROWS = 32
 BANK = 512
 OUT_RANGES = (
-    ((0, 512), (512, 1280), (1280, 2048)),
+    ((0, 256), (256, 768), (768, 1408), (1408, 2048)),
     ((0, 768), (768, 1536), (1536, 1920), (1920, 2048)),
 )
-AT_WORDS0, AT_RAW11, AT_RES0, AT_WORDS1, AT_RES1 = 0, 0, 2048, 10240, 10240
+AT_SUMS, AT_WORDS0, AT_RAW11, AT_RES0, AT_WORDS1, AT_RES1 = 0, 2496, 2496, 4544, 12736, 12736
 
 
 def tile_picked_unmerge_relu_p_kernel(tc, x_words, x_scales, w1, res, offs, own, out):
@@ -70,8 +70,8 @@ def tile_picked_unmerge_relu_p_kernel(tc, x_words, x_scales, w1, res, offs, own,
             res_sb[b, lo] = sbuf([P, hi - lo], F32, "res%d_%d" % (b, lo), after, at)
             nc.sync.dma_start(res_sb[b, lo][:], res[b * P : (b + 1) * P, lo:hi])
 
-        def round_w(b, passes, after=None):
-            rounded = sbuf([P, len(passes), P, PACK], BF16, "rounded%d%d" % (b, passes[0]), after)
+        def round_w(b, passes, after=None, at=None):
+            rounded = sbuf([P, len(passes), P, PACK], BF16, "rounded%d%d" % (b, passes[0]), after, at)
             for n, z in enumerate(passes):
                 nc.scalar.activation(
                     rounded[:, n, :, :].rearrange("p (c i) t -> p c t i", i=LINE),
@@ -142,9 +142,10 @@ def tile_picked_unmerge_relu_p_kernel(tc, x_words, x_scales, w1, res, offs, own,
         load_w(1, 0, after="scales")
 
         pick_words(0, 0, S)
-        load_w(1, 1, at=AT_RAW11)
-        for lo, hi in OUT_RANGES[0]:
+        for lo, hi in OUT_RANGES[0][:2]:
             load_res(0, lo, hi, at=AT_RES0 + 4 * lo)
+        load_w(1, 1, at=AT_RAW11)
+        load_res(0, OUT_RANGES[0][2][0], U, at=AT_RES0 + 4 * OUT_RANGES[0][2][0])
 
         pick_words(1, *PICK_RANGES[0])
         quantize_w(0, (0,), round_w(0, (0,)))
@@ -163,12 +164,17 @@ def tile_picked_unmerge_relu_p_kernel(tc, x_words, x_scales, w1, res, offs, own,
             product(acc[:], 0, 1, lo, hi)
             nc.vector.tensor_scalar_max(y0[:, lo:hi], acc[:], 0.0)
 
-        quantize_w(1, (0, 1), round_w(1, (0, 1)), after="w_codes01")
-        for lo, hi in PICK_RANGES:
-            acc = psum.tile([P, hi - lo], F32, name="acc1_%d" % lo)
-            for z in range(PASSES):
-                product(acc[:], 1, z, lo, hi)
+        quantize_w(1, (0,), round_w(1, (0,)), after="w_codes01")
+        accs = [psum.tile([P, hi - lo], F32, name="acc1_%d" % lo) for lo, hi in PICK_RANGES]
+        for acc, (lo, hi) in zip(accs, PICK_RANGES):
+            product(acc[:], 1, 0, lo, hi)
+        unmerge(0, y0, 0)
+        unmerge(0, y0, 1)
+        quantize_w(1, (1,), round_w(1, (1,), at=AT_RES0))
+        for acc, (lo, hi) in zip(accs, PICK_RANGES):
+            product(acc[:], 1, 1, lo, hi)
             nc.scalar.activation(y1[:, lo:hi], acc[:], RELU)
-        for b, y in enumerate((y0, y1)):
-            for n in range(len(OUT_RANGES[b])):
-                unmerge(b, y, n)
+        unmerge(0, y0, 2, at=AT_SUMS)
+        unmerge(0, y0, 3)
+        for n in range(len(OUT_RANGES[1])):
+            unmerge(1, y1, n)

@@ -142,6 +142,17 @@ def tile_picked_unmerge_relu_p_kernel(tc, x_words, x_scales, w1, res, offs, own,
         load_w(1, 0, after="scales")
 
         pick_words(0, 0, S)
+        unread = psum.tile([P, BANK], F32, name="unread")
+        for lo in range(0, S, BANK):
+            nc.tensor.matmul_mx(
+                out=unread[:],
+                lhsT=picked_words[0, 0][:, :P].bitcast(FP8X4),
+                lhsT_scale=picked_scales[:, :P],
+                rhs=picked_words[0, 0][:, lo : lo + BANK].bitcast(FP8X4),
+                rhs_scale=picked_scales[:, lo : lo + BANK],
+                start=True,
+                stop=True,
+            )
         for lo, hi in OUT_RANGES[0][:2]:
             load_res(0, lo, hi, at=AT_RES0 + 4 * lo)
         load_w(1, 1, at=AT_RAW11)
@@ -157,7 +168,7 @@ def tile_picked_unmerge_relu_p_kernel(tc, x_words, x_scales, w1, res, offs, own,
 
         y0 = sbuf([P, S], F32, "y0")
         y1 = sbuf([P, S], F32, "y1")
-        accs = [psum.tile([P, hi - lo], F32, name="acc0_%d" % lo) for lo, hi in CHUNKS]
+        accs = [psum.tile([P, hi - lo], F32, name="acc0_%d" % lo, tag="acc_%d" % lo) for lo, hi in CHUNKS]
         for acc, (lo, hi) in zip(accs, CHUNKS):
             product(acc[:], 0, 0, lo, hi)
         for acc, (lo, hi) in zip(accs, CHUNKS):
@@ -165,13 +176,13 @@ def tile_picked_unmerge_relu_p_kernel(tc, x_words, x_scales, w1, res, offs, own,
             nc.vector.tensor_scalar_max(y0[:, lo:hi], acc[:], 0.0)
 
         quantize_w(1, (0,), round_w(1, (0,)), after="w_codes01")
-        accs = [psum.tile([P, hi - lo], F32, name="acc1_%d" % lo) for lo, hi in PICK_RANGES]
-        for acc, (lo, hi) in zip(accs, PICK_RANGES):
+        accs = [psum.tile([P, hi - lo], F32, name="acc1_%d" % lo, tag="acc_%d" % lo) for lo, hi in CHUNKS]
+        for acc, (lo, hi) in zip(accs, CHUNKS):
             product(acc[:], 1, 0, lo, hi)
         unmerge(0, y0, 0)
         unmerge(0, y0, 1)
         quantize_w(1, (1,), round_w(1, (1,), at=AT_RES0))
-        for acc, (lo, hi) in zip(accs, PICK_RANGES):
+        for acc, (lo, hi) in zip(accs, CHUNKS):
             product(acc[:], 1, 1, lo, hi)
             nc.scalar.activation(y1[:, lo:hi], acc[:], RELU)
         unmerge(0, y0, 2, at=AT_SUMS)

@@ -24,13 +24,13 @@ ROW_BLOCKS = N // P
 ENTRIES_PER_COLUMN = 16
 LINE = 4
 
-PICK_RANGES = ((0, 512), (512, 768), (768, 1024))
+PICK_RANGES = ((0, 768), (768, 1024))
 CHUNKS = ((0, 256), (256, 512), (512, 768), (768, 896), (896, 1024))
 SCALE_ROWS = 32
 BANK = 512
 OUT_RANGES = (
     ((0, 256), (256, 768), (768, 1408), (1408, 2048)),
-    ((0, 768), (768, 1536), (1536, 1920), (1920, 2048)),
+    ((0, 960), (960, 1600), (1600, 1920), (1920, 2048)),
 )
 AT_SUMS, AT_WORDS0, AT_RAW11, AT_RES0, AT_WORDS1, AT_RES1 = 0, 2496, 2496, 4544, 12736, 12736
 
@@ -150,8 +150,8 @@ def tile_picked_unmerge_relu_p_kernel(tc, x_words, x_scales, w1, res, offs, own,
                 lhsT_scale=picked_scales[:, :P],
                 rhs=picked_words[0, 0][:, lo : lo + BANK].bitcast(FP8X4),
                 rhs_scale=picked_scales[:, lo : lo + BANK],
-                start=True,
-                stop=True,
+                start=(lo == 0),
+                stop=(lo > 0),
             )
         for lo, hi in OUT_RANGES[0][:2]:
             load_res(0, lo, hi, at=AT_RES0 + 4 * lo)
@@ -162,20 +162,23 @@ def tile_picked_unmerge_relu_p_kernel(tc, x_words, x_scales, w1, res, offs, own,
         quantize_w(0, (0,), round_w(0, (0,)))
         pick_words(1, *PICK_RANGES[1], after="raw00")
         quantize_w(0, (1,), round_w(0, (1,)))
-        pick_words(1, *PICK_RANGES[2], after="raw01")
+        rounded10 = round_w(1, (0,))
         load_res(1, 0, OUT_RANGES[1][0][1], at=AT_RES1)
         load_res(1, OUT_RANGES[1][0][1], U, at=AT_RES1 + 4 * OUT_RANGES[1][0][1])
 
-        y0 = sbuf([P, S], F32, "y0")
+        y0 = sbuf([P, S], F32, "y0", after="scales")
         y1 = sbuf([P, S], F32, "y1")
         accs = [psum.tile([P, hi - lo], F32, name="acc0_%d" % lo, tag="acc_%d" % lo) for lo, hi in CHUNKS]
         for acc, (lo, hi) in zip(accs, CHUNKS):
             product(acc[:], 0, 0, lo, hi)
-        for acc, (lo, hi) in zip(accs, CHUNKS):
-            product(acc[:], 0, 1, lo, hi)
-            nc.vector.tensor_scalar_max(y0[:, lo:hi], acc[:], 0.0)
+        for c, (lo, hi) in enumerate(CHUNKS):
+            product(accs[c][:], 0, 1, lo, hi)
+            if c < 2:
+                nc.scalar.activation(y0[:, lo:hi], accs[c][:], RELU)
+            else:
+                nc.vector.tensor_scalar_max(y0[:, lo:hi], accs[c][:], 0.0)
 
-        quantize_w(1, (0,), round_w(1, (0,)), after="w_codes01")
+        quantize_w(1, (0,), rounded10, after="w_codes01")
         accs = [psum.tile([P, hi - lo], F32, name="acc1_%d" % lo, tag="acc_%d" % lo) for lo, hi in CHUNKS]
         for acc, (lo, hi) in zip(accs, CHUNKS):
             product(acc[:], 1, 0, lo, hi)

@@ -24,7 +24,8 @@ ROW_BLOCKS = N // P
 ENTRIES_PER_COLUMN = 16
 LINE = 4
 
-PICK_RANGES = ((0, 768), (768, 1024))
+PICK_RANGES = ((0, 512), (512, 768), (768, 1024))
+WARM_AFTER = 640
 CHUNKS = ((0, 256), (256, 512), (512, 768), (768, 896), (896, 1024))
 SCALE_ROWS = 32
 BANK = 512
@@ -141,9 +142,11 @@ def tile_picked_unmerge_relu_p_kernel(tc, x_words, x_scales, w1, res, offs, own,
             )
         load_w(1, 0, after="scales")
 
-        pick_words(0, 0, S)
+        picked_words[0, 0] = sbuf([P, S], U32, "picked_words0_0")
+        for lo, hi in ((0, WARM_AFTER), (WARM_AFTER, S)):
+            nc.vector.tensor_copy(picked_words[0, 0][:, lo:hi], words[0][:].bitcast(U32).indirect(entries(offs_sb, lo, hi)))
         unread = psum.tile([P, BANK], F32, name="unread")
-        for lo in range(0, S, BANK):
+        for lo in (0, WARM_AFTER - BANK):
             nc.tensor.matmul_mx(
                 out=unread[:],
                 lhsT=picked_words[0, 0][:, :P].bitcast(FP8X4),
@@ -162,6 +165,7 @@ def tile_picked_unmerge_relu_p_kernel(tc, x_words, x_scales, w1, res, offs, own,
         quantize_w(0, (0,), round_w(0, (0,)))
         pick_words(1, *PICK_RANGES[1], after="raw00")
         quantize_w(0, (1,), round_w(0, (1,)))
+        pick_words(1, *PICK_RANGES[2], after="raw01")
         rounded10 = round_w(1, (0,))
         load_res(1, 0, OUT_RANGES[1][0][1], at=AT_RES1)
         load_res(1, OUT_RANGES[1][0][1], U, at=AT_RES1 + 4 * OUT_RANGES[1][0][1])

@@ -24,8 +24,7 @@ ROW_BLOCKS = N // P
 ENTRIES_PER_COLUMN = 16
 LINE = 4
 
-PICK_RANGES = ((0, 512), (512, 768), (768, 1024))
-WARM_AFTER = 640
+PICK_RANGES = ((0, 256), (256, 512), (512, 768), (768, 1024))
 CHUNKS = ((0, 256), (256, 512), (512, 768), (768, 896), (896, 1024))
 SCALE_ROWS = 32
 BANK = 512
@@ -128,10 +127,10 @@ def tile_picked_unmerge_relu_p_kernel(tc, x_words, x_scales, w1, res, offs, own,
         nc.sync.dma_start(scales[P - SCALE_ROWS :, :].bitcast(I32), x_scales.rearrange("z r n -> r z n").bitcast(I32))
         nc.sync.dma_start(offs_sb[:], offs)
         load_words(0)
-        nc.sync.dma_start(own_sb[:], own)
         load_words(1)
         load_w(0, 0)
         load_w(0, 1)
+        nc.sync.dma_start(own_sb[:], own)
 
         nc.vector.tensor_copy(picked_scales[:], scales[:].indirect(offs_sb[:]))
         for q in (0, 2, 1, 3):
@@ -142,30 +141,29 @@ def tile_picked_unmerge_relu_p_kernel(tc, x_words, x_scales, w1, res, offs, own,
             )
         load_w(1, 0, after="scales")
 
-        picked_words[0, 0] = sbuf([P, S], U32, "picked_words0_0")
-        for lo, hi in ((0, WARM_AFTER), (WARM_AFTER, S)):
-            nc.vector.tensor_copy(picked_words[0, 0][:, lo:hi], words[0][:].bitcast(U32).indirect(entries(offs_sb, lo, hi)))
-        unread = psum.tile([P, BANK], F32, name="unread")
-        for lo in (0, WARM_AFTER - BANK):
-            nc.tensor.matmul_mx(
-                out=unread[:],
-                lhsT=picked_words[0, 0][:, :P].bitcast(FP8X4),
-                lhsT_scale=picked_scales[:, :P],
-                rhs=picked_words[0, 0][:, lo : lo + BANK].bitcast(FP8X4),
-                rhs_scale=picked_scales[:, lo : lo + BANK],
-                start=(lo == 0),
-                stop=(lo > 0),
-            )
+        pick_words(0, 0, S)
         for lo, hi in OUT_RANGES[0][:2]:
             load_res(0, lo, hi, at=AT_RES0 + 4 * lo)
         load_w(1, 1, at=AT_RAW11)
         load_res(0, OUT_RANGES[0][2][0], U, at=AT_RES0 + 4 * OUT_RANGES[0][2][0])
 
         pick_words(1, *PICK_RANGES[0])
+        unread = psum.tile([P, BANK], F32, name="unread")
+        for lo in range(0, S, BANK):
+            nc.tensor.matmul_mx(
+                out=unread[:],
+                lhsT=picked_words[1, 0][:, :P].bitcast(FP8X4),
+                lhsT_scale=picked_scales[:, :P],
+                rhs=picked_words[0, 0][:, lo : lo + BANK].bitcast(FP8X4),
+                rhs_scale=picked_scales[:, lo : lo + BANK],
+                start=(lo == 0),
+                stop=(lo > 0),
+            )
+        pick_words(1, *PICK_RANGES[1])
         quantize_w(0, (0,), round_w(0, (0,)))
-        pick_words(1, *PICK_RANGES[1], after="raw00")
+        pick_words(1, *PICK_RANGES[2], after="raw00")
         quantize_w(0, (1,), round_w(0, (1,)))
-        pick_words(1, *PICK_RANGES[2], after="raw01")
+        pick_words(1, *PICK_RANGES[3], after="raw01")
         rounded10 = round_w(1, (0,))
         load_res(1, 0, OUT_RANGES[1][0][1], at=AT_RES1)
         load_res(1, OUT_RANGES[1][0][1], U, at=AT_RES1 + 4 * OUT_RANGES[1][0][1])

@@ -20,19 +20,28 @@ P = 128
 PACK = 4
 PASSES = K // (P * PACK)
 QUADRANT = 32
-ROW_BLOCKS = N // P
+SCALE_ROWS = K // 32
 ENTRIES_PER_COLUMN = 16
 LINE = 4
-
-PICK_RANGES = ((0, 256), (256, 512), (512, 768), (768, 1024))
-CHUNKS = ((0, 256), (256, 512), (512, 768), (768, 896), (896, 1024))
-SCALE_ROWS = 32
 BANK = 512
+WORD_BYTES = 4
+ALIGN = 64
+
+PICK_RANGES = ((0, 512), (512, 768), (768, 1024))
+CHUNKS = ((0, 256), (256, 512), (512, 768), (768, 896), (896, 1024))
+SCALAR_CHUNKS = 2
 OUT_RANGES = (
     ((0, 256), (256, 768), (768, 1408), (1408, 2048)),
     ((0, 960), (960, 1600), (1600, 1920), (1920, 2048)),
 )
-AT_SUMS, AT_WORDS0, AT_RAW11, AT_RES0, AT_WORDS1, AT_RES1 = 0, 2496, 2496, 4544, 12736, 12736
+MOVE_ORDER = (0, 2, 1, 3)
+
+AT_THIRD_SUMS = 0
+AT_WORDS0 = WORD_BYTES * (OUT_RANGES[0][2][1] - OUT_RANGES[0][2][0]) - ALIGN
+AT_LAST_QUARTER = AT_WORDS0
+AT_RES0 = AT_LAST_QUARTER + WORD_BYTES * PACK * P
+AT_WORDS1 = AT_RES0 + WORD_BYTES * U
+AT_RES1 = AT_WORDS1
 
 
 def tile_picked_unmerge_relu_p_kernel(tc, x_words, x_scales, w1, res, offs, own, out):
@@ -44,8 +53,8 @@ def tile_picked_unmerge_relu_p_kernel(tc, x_words, x_scales, w1, res, offs, own,
 
         def sbuf(shape, dtype, name, after=None, at=None):
             if at is not None:
-                return laid.tile(shape, dtype, name=name, tag=name, align_bytes=64, offset=at)
-            return keep.tile(shape, dtype, name=name, tag=after or name, align_bytes=64)
+                return laid.tile(shape, dtype, name=name, tag=name, align_bytes=ALIGN, offset=at)
+            return keep.tile(shape, dtype, name=name, tag=after or name, align_bytes=ALIGN)
 
         def entries(list_tile, lo, hi):
             return list_tile[:, lo // ENTRIES_PER_COLUMN : hi // ENTRIES_PER_COLUMN]
@@ -56,7 +65,9 @@ def tile_picked_unmerge_relu_p_kernel(tc, x_words, x_scales, w1, res, offs, own,
         scales = sbuf([P, T], U8, "scales")
         picked_scales = sbuf([P, S], U8, "picked_scales")
         placed_scales = sbuf([P, PASSES * S], U8, "placed_scales")
-        w_raw, w_codes, w_scales, picked_words, res_sb = {}, {}, {}, {}, {}
+        w_raw, w_codes, w_scales = {}, {}, {}
+        picked_words = {}
+        res_sb = {}
 
         def load_words(z):
             nc.sync.dma_start(words[z][:], x_words[z].rearrange("p n t -> p (n t)").bitcast(I32))
@@ -66,43 +77,41 @@ def tile_picked_unmerge_relu_p_kernel(tc, x_words, x_scales, w1, res, offs, own,
             rows = w1[z * P * PACK : (z + 1) * P * PACK, b * P : (b + 1) * P]
             nc.sync.dma_start(w_raw[b, z][:], rows.rearrange("(p t) m -> p t m", t=PACK))
 
-        def load_res(b, lo, hi, after=None, at=None):
-            res_sb[b, lo] = sbuf([P, hi - lo], F32, "res%d_%d" % (b, lo), after, at)
+        def load_res(b, lo, hi):
+            res_sb[b, lo] = sbuf([P, hi - lo], F32, "res%d_%d" % (b, lo), at=(AT_RES0, AT_RES1)[b] + WORD_BYTES * lo)
             nc.sync.dma_start(res_sb[b, lo][:], res[b * P : (b + 1) * P, lo:hi])
 
-        def round_w(b, passes, after=None, at=None):
-            rounded = sbuf([P, len(passes), P, PACK], BF16, "rounded%d%d" % (b, passes[0]), after, at)
-            for n, z in enumerate(passes):
-                nc.scalar.activation(
-                    rounded[:, n, :, :].rearrange("p (c i) t -> p c t i", i=LINE),
-                    w_raw[b, z][:].rearrange("p t (c i) -> p c t i", i=LINE),
-                    COPY,
-                )
+        def round_w(b, z, at=None):
+            rounded = sbuf([P, P, PACK], BF16, "rounded%d%d" % (b, z), at=at)
+            nc.scalar.activation(
+                rounded[:].rearrange("p (c i) t -> p c t i", i=LINE),
+                w_raw[b, z][:].rearrange("p t (c i) -> p c t i", i=LINE),
+                COPY,
+            )
             return rounded
 
-        def quantize_w(b, passes, rounded, after=None):
-            codes = sbuf([P, len(passes) * P], U32, "w_codes%d%d" % (b, passes[0]), after)
-            scale_bytes = sbuf([P, len(passes) * P], U8, "w_scales%d%d" % (b, passes[0]))
+        def quantize_w(b, z, rounded, after=None):
+            w_codes[b, z] = sbuf([P, P], U32, "w_codes%d%d" % (b, z), after)
+            w_scales[b, z] = sbuf([P, P], U8, "w_scales%d%d" % (b, z))
             nc.vector.quantize_mx(
-                out=codes[:].bitcast(FP8X4),
-                scales=scale_bytes[:],
-                in_=rounded[:].rearrange("p n m t -> p (n m t)"),
+                out=w_codes[b, z][:].bitcast(FP8X4),
+                scales=w_scales[b, z][:],
+                in_=rounded[:].rearrange("p m t -> p (m t)"),
             )
-            for n, z in enumerate(passes):
-                w_codes[b, z] = codes[:, n * P : (n + 1) * P]
-                w_scales[b, z] = scale_bytes[:, n * P : (n + 1) * P]
 
         def pick_words(z, lo, hi, after=None):
-            dst = sbuf([P, hi - lo], U32, "picked_words%d_%d" % (z, lo), after)
-            picked_words[z, lo] = dst
-            nc.vector.tensor_copy(dst[:], words[z][:].bitcast(U32).indirect(entries(offs_sb, lo, hi)))
+            picked_words[z, lo] = sbuf([P, hi - lo], U32, "picked_words%d_%d" % (z, lo), after)
+            nc.vector.tensor_copy(picked_words[z, lo][:], words[z][:].bitcast(U32).indirect(entries(offs_sb, lo, hi)))
+
+        def accumulators(b):
+            return [psum.tile([P, hi - lo], F32, name="acc%d_%d" % (b, lo), tag="acc_%d" % lo) for lo, hi in CHUNKS]
 
         def product(acc, b, z, lo, hi):
             first = max(start for pass_of_tile, start in picked_words if pass_of_tile == z and start <= lo)
             nc.tensor.matmul_mx(
-                out=acc,
-                lhsT=w_codes[b, z].bitcast(FP8X4),
-                lhsT_scale=w_scales[b, z],
+                out=acc[:],
+                lhsT=w_codes[b, z][:].bitcast(FP8X4),
+                lhsT_scale=w_scales[b, z][:],
                 rhs=picked_words[z, first][:, lo - first : hi - first].bitcast(FP8X4),
                 rhs_scale=placed_scales[:, z * S + lo : z * S + hi],
                 start=(z == 0),
@@ -121,10 +130,11 @@ def tile_picked_unmerge_relu_p_kernel(tc, x_words, x_scales, w1, res, offs, own,
             )
             nc.sync.dma_start(out[b * P : (b + 1) * P, lo:hi], sums[:])
 
-        nc.vector.memset(scales[: P - SCALE_ROWS, :].bitcast(I32), 0)
+        first_row = P - SCALE_ROWS
+        nc.vector.memset(scales[:first_row, :].bitcast(I32), 0)
         nc.vector.memset(placed_scales[:].bitcast(I32), 0)
 
-        nc.sync.dma_start(scales[P - SCALE_ROWS :, :].bitcast(I32), x_scales.rearrange("z r n -> r z n").bitcast(I32))
+        nc.sync.dma_start(scales[first_row:, :].bitcast(I32), x_scales.rearrange("z r n -> r z n").bitcast(I32))
         nc.sync.dma_start(offs_sb[:], offs)
         load_words(0)
         load_words(1)
@@ -133,8 +143,8 @@ def tile_picked_unmerge_relu_p_kernel(tc, x_words, x_scales, w1, res, offs, own,
         nc.sync.dma_start(own_sb[:], own)
 
         nc.vector.tensor_copy(picked_scales[:], scales[:].indirect(offs_sb[:]))
-        for q in (0, 2, 1, 3):
-            row = P - SCALE_ROWS + PASSES * PACK * q
+        for q in MOVE_ORDER:
+            row = first_row + PASSES * PACK * q
             nc.sync.dma_start(
                 placed_scales[QUADRANT * q : QUADRANT * q + PACK, :].bitcast(I32),
                 picked_scales[row : row + PASSES * PACK, :].bitcast(I32),
@@ -143,54 +153,53 @@ def tile_picked_unmerge_relu_p_kernel(tc, x_words, x_scales, w1, res, offs, own,
 
         pick_words(0, 0, S)
         for lo, hi in OUT_RANGES[0][:2]:
-            load_res(0, lo, hi, at=AT_RES0 + 4 * lo)
-        load_w(1, 1, at=AT_RAW11)
-        load_res(0, OUT_RANGES[0][2][0], U, at=AT_RES0 + 4 * OUT_RANGES[0][2][0])
+            load_res(0, lo, hi)
+        load_w(1, 1, at=AT_LAST_QUARTER)
+        load_res(0, OUT_RANGES[0][2][0], U)
 
         pick_words(1, *PICK_RANGES[0])
         unread = psum.tile([P, BANK], F32, name="unread")
         for lo in range(0, S, BANK):
             nc.tensor.matmul_mx(
                 out=unread[:],
-                lhsT=picked_words[1, 0][:, :P].bitcast(FP8X4),
+                lhsT=picked_words[0, 0][:, :P].bitcast(FP8X4),
                 lhsT_scale=picked_scales[:, :P],
                 rhs=picked_words[0, 0][:, lo : lo + BANK].bitcast(FP8X4),
                 rhs_scale=picked_scales[:, lo : lo + BANK],
                 start=(lo == 0),
-                stop=(lo > 0),
+                stop=(lo + BANK == S),
             )
-        pick_words(1, *PICK_RANGES[1])
-        quantize_w(0, (0,), round_w(0, (0,)))
-        pick_words(1, *PICK_RANGES[2], after="raw00")
-        quantize_w(0, (1,), round_w(0, (1,)))
-        pick_words(1, *PICK_RANGES[3], after="raw01")
-        rounded10 = round_w(1, (0,))
-        load_res(1, 0, OUT_RANGES[1][0][1], at=AT_RES1)
-        load_res(1, OUT_RANGES[1][0][1], U, at=AT_RES1 + 4 * OUT_RANGES[1][0][1])
+        quantize_w(0, 0, round_w(0, 0))
+        pick_words(1, *PICK_RANGES[1], after="raw00")
+        quantize_w(0, 1, round_w(0, 1))
+        pick_words(1, *PICK_RANGES[2], after="raw01")
+        rounded10 = round_w(1, 0)
+        load_res(1, 0, OUT_RANGES[1][0][1])
+        load_res(1, OUT_RANGES[1][0][1], U)
 
         y0 = sbuf([P, S], F32, "y0", after="scales")
         y1 = sbuf([P, S], F32, "y1")
-        accs = [psum.tile([P, hi - lo], F32, name="acc0_%d" % lo, tag="acc_%d" % lo) for lo, hi in CHUNKS]
-        for acc, (lo, hi) in zip(accs, CHUNKS):
-            product(acc[:], 0, 0, lo, hi)
+        accs0 = accumulators(0)
+        for acc, (lo, hi) in zip(accs0, CHUNKS):
+            product(acc, 0, 0, lo, hi)
         for c, (lo, hi) in enumerate(CHUNKS):
-            product(accs[c][:], 0, 1, lo, hi)
-            if c < 2:
-                nc.scalar.activation(y0[:, lo:hi], accs[c][:], RELU)
+            product(accs0[c], 0, 1, lo, hi)
+            if c < SCALAR_CHUNKS:
+                nc.scalar.activation(y0[:, lo:hi], accs0[c][:], RELU)
             else:
-                nc.vector.tensor_scalar_max(y0[:, lo:hi], accs[c][:], 0.0)
+                nc.vector.tensor_scalar_max(y0[:, lo:hi], accs0[c][:], 0.0)
 
-        quantize_w(1, (0,), rounded10, after="w_codes01")
-        accs = [psum.tile([P, hi - lo], F32, name="acc1_%d" % lo, tag="acc_%d" % lo) for lo, hi in CHUNKS]
-        for acc, (lo, hi) in zip(accs, CHUNKS):
-            product(acc[:], 1, 0, lo, hi)
+        quantize_w(1, 0, rounded10, after="w_codes01")
+        accs1 = accumulators(1)
+        for acc, (lo, hi) in zip(accs1, CHUNKS):
+            product(acc, 1, 0, lo, hi)
         unmerge(0, y0, 0)
         unmerge(0, y0, 1)
-        quantize_w(1, (1,), round_w(1, (1,), at=AT_RES0))
-        for acc, (lo, hi) in zip(accs, CHUNKS):
-            product(acc[:], 1, 1, lo, hi)
+        quantize_w(1, 1, round_w(1, 1, at=AT_RES0))
+        for acc, (lo, hi) in zip(accs1, CHUNKS):
+            product(acc, 1, 1, lo, hi)
             nc.scalar.activation(y1[:, lo:hi], acc[:], RELU)
-        unmerge(0, y0, 2, at=AT_SUMS)
+        unmerge(0, y0, 2, at=AT_THIRD_SUMS)
         unmerge(0, y0, 3)
         for n in range(len(OUT_RANGES[1])):
             unmerge(1, y1, n)

@@ -31,7 +31,7 @@ PICK_RANGES = ((0, 512), (512, 768), (768, 1024))
 CHUNKS = ((0, 256), (256, 512), (512, 768), (768, 896), (896, 1024))
 SCALAR_CHUNKS = 2
 OUT_RANGES = (
-    ((0, 256), (256, 768), (768, 1408), (1408, 2048)),
+    ((0, 256), (256, 896), (896, 1472), (1472, 2048)),
     ((0, 960), (960, 1600), (1600, 1920), (1920, 2048)),
 )
 MOVE_ORDER = (0, 2, 1, 3)
@@ -155,7 +155,8 @@ def tile_picked_unmerge_relu_p_kernel(tc, x_words, x_scales, w1, res, offs, own,
         for lo, hi in OUT_RANGES[0][:2]:
             load_res(0, lo, hi)
         load_w(1, 1, at=AT_LAST_QUARTER)
-        load_res(0, OUT_RANGES[0][2][0], U)
+        for lo, hi in OUT_RANGES[0][2:]:
+            load_res(0, lo, hi)
 
         pick_words(1, *PICK_RANGES[0])
         unread = psum.tile([P, BANK], F32, name="unread")

@@ -27,21 +27,33 @@ BANK = 512
 WORD_BYTES = 4
 ALIGN = 64
 
-PICK_RANGES = ((0, 512), (512, 768), (768, 1024))
+PICK_RANGES = (((0, 512), (512, 1024)), ((0, 768), (768, 1024)))
 CHUNKS = ((0, 256), (256, 512), (512, 768), (768, 896), (896, 1024))
-SCALAR_CHUNKS = 2
+VECTOR_CHUNKS = (2, 4)
 OUT_RANGES = (
-    ((0, 256), (256, 896), (896, 1472), (1472, 2048)),
+    ((0, 384), (384, 896), (896, 1472), (1472, 2048)),
     ((0, 960), (960, 1600), (1600, 1920), (1920, 2048)),
 )
 MOVE_ORDER = (0, 2, 1, 3)
 
-AT_THIRD_SUMS = 0
-AT_WORDS0 = WORD_BYTES * (OUT_RANGES[0][2][1] - OUT_RANGES[0][2][0]) - ALIGN
-AT_LAST_QUARTER = AT_WORDS0
-AT_RES0 = AT_LAST_QUARTER + WORD_BYTES * PACK * P
-AT_WORDS1 = AT_RES0 + WORD_BYTES * U
-AT_RES1 = AT_WORDS1
+
+def width(b, n):
+    return WORD_BYTES * (OUT_RANGES[b][n][1] - OUT_RANGES[b][n][0])
+
+
+QUARTER = WORD_BYTES * PACK * P
+TABLE = WORD_BYTES * T
+AT_SECOND_SUMS = 0
+AT_RAW10 = AT_SECOND_SUMS + width(0, 1) - ALIGN
+AT_WORDS0 = AT_RAW10 + QUARTER - ALIGN
+AT_RES00 = AT_WORDS0 + ALIGN
+AT_RES01 = AT_RES00 + width(0, 0)
+AT_RAW11 = AT_WORDS0 + TABLE - ALIGN
+AT_THIRD_SUMS = AT_RAW11 + QUARTER - ALIGN
+AT_RES02 = AT_THIRD_SUMS + width(0, 2)
+AT_WORDS1 = AT_RES02 + width(0, 2) - ALIGN
+AT_RES03 = AT_WORDS1 + ALIGN
+AT_RES1 = AT_RES03 + width(0, 3)
 
 
 def tile_picked_unmerge_relu_p_kernel(tc, x_words, x_scales, w1, res, offs, own, out):
@@ -64,10 +76,11 @@ def tile_picked_unmerge_relu_p_kernel(tc, x_words, x_scales, w1, res, offs, own,
         words = [sbuf([P, T], I32, "words0", at=AT_WORDS0), sbuf([P, T], I32, "words1", at=AT_WORDS1)]
         scales = sbuf([P, T], U8, "scales")
         picked_scales = sbuf([P, S], U8, "picked_scales")
-        placed_scales = sbuf([P, PASSES * S], U8, "placed_scales")
+        placed_scales = [sbuf([P, S], U8, "placed_scales%d" % z) for z in range(PASSES)]
         w_raw, w_codes, w_scales = {}, {}, {}
         picked_words = {}
         res_sb = {}
+        first_row = P - SCALE_ROWS
 
         def load_words(z):
             nc.sync.dma_start(words[z][:], x_words[z].rearrange("p n t -> p (n t)").bitcast(I32))
@@ -77,12 +90,20 @@ def tile_picked_unmerge_relu_p_kernel(tc, x_words, x_scales, w1, res, offs, own,
             rows = w1[z * P * PACK : (z + 1) * P * PACK, b * P : (b + 1) * P]
             nc.sync.dma_start(w_raw[b, z][:], rows.rearrange("(p t) m -> p t m", t=PACK))
 
-        def load_res(b, lo, hi):
-            res_sb[b, lo] = sbuf([P, hi - lo], F32, "res%d_%d" % (b, lo), at=(AT_RES0, AT_RES1)[b] + WORD_BYTES * lo)
+        def load_res(b, lo, hi, at):
+            res_sb[b, lo] = sbuf([P, hi - lo], F32, "res%d_%d" % (b, lo), at=at)
             nc.sync.dma_start(res_sb[b, lo][:], res[b * P : (b + 1) * P, lo:hi])
 
-        def round_w(b, z, at=None):
-            rounded = sbuf([P, P, PACK], BF16, "rounded%d%d" % (b, z), at=at)
+        def place_scales(z):
+            for q in MOVE_ORDER:
+                row = first_row + z * SCALE_ROWS // PASSES + PACK * q
+                nc.sync.dma_start(
+                    placed_scales[z][QUADRANT * q : QUADRANT * q + PACK, :].bitcast(I32),
+                    picked_scales[row : row + PACK, :].bitcast(I32),
+                )
+
+        def round_w(b, z, after=None):
+            rounded = sbuf([P, P, PACK], BF16, "rounded%d%d" % (b, z), after)
             nc.scalar.activation(
                 rounded[:].rearrange("p (c i) t -> p c t i", i=LINE),
                 w_raw[b, z][:].rearrange("p t (c i) -> p c t i", i=LINE),
@@ -90,8 +111,8 @@ def tile_picked_unmerge_relu_p_kernel(tc, x_words, x_scales, w1, res, offs, own,
             )
             return rounded
 
-        def quantize_w(b, z, rounded, after=None):
-            w_codes[b, z] = sbuf([P, P], U32, "w_codes%d%d" % (b, z), after)
+        def quantize_w(b, z, rounded):
+            w_codes[b, z] = sbuf([P, P], U32, "w_codes%d%d" % (b, z))
             w_scales[b, z] = sbuf([P, P], U8, "w_scales%d%d" % (b, z))
             nc.vector.quantize_mx(
                 out=w_codes[b, z][:].bitcast(FP8X4),
@@ -113,7 +134,7 @@ def tile_picked_unmerge_relu_p_kernel(tc, x_words, x_scales, w1, res, offs, own,
                 lhsT=w_codes[b, z][:].bitcast(FP8X4),
                 lhsT_scale=w_scales[b, z][:],
                 rhs=picked_words[z, first][:, lo - first : hi - first].bitcast(FP8X4),
-                rhs_scale=placed_scales[:, z * S + lo : z * S + hi],
+                rhs_scale=placed_scales[z][:, lo:hi],
                 start=(z == 0),
                 stop=(z == PASSES - 1),
             )
@@ -130,73 +151,69 @@ def tile_picked_unmerge_relu_p_kernel(tc, x_words, x_scales, w1, res, offs, own,
             )
             nc.sync.dma_start(out[b * P : (b + 1) * P, lo:hi], sums[:])
 
-        first_row = P - SCALE_ROWS
         nc.vector.memset(scales[:first_row, :].bitcast(I32), 0)
-        nc.vector.memset(placed_scales[:].bitcast(I32), 0)
+        for z in range(PASSES):
+            nc.vector.memset(placed_scales[z][:].bitcast(I32), 0)
 
-        nc.sync.dma_start(scales[first_row:, :].bitcast(I32), x_scales.rearrange("z r n -> r z n").bitcast(I32))
+        nc.sync.dma_start(scales[first_row:, :].bitcast(I32), x_scales.rearrange("z r n -> (z r) n").bitcast(I32))
         nc.sync.dma_start(offs_sb[:], offs)
         load_words(0)
-        load_words(1)
         load_w(0, 0)
-        load_w(0, 1)
+        load_words(1)
         nc.sync.dma_start(own_sb[:], own)
 
         nc.vector.tensor_copy(picked_scales[:], scales[:].indirect(offs_sb[:]))
-        for q in MOVE_ORDER:
-            row = first_row + PASSES * PACK * q
-            nc.sync.dma_start(
-                placed_scales[QUADRANT * q : QUADRANT * q + PACK, :].bitcast(I32),
-                picked_scales[row : row + PASSES * PACK, :].bitcast(I32),
-            )
-        load_w(1, 0, after="scales")
+        place_scales(0)
+        load_w(0, 1, after="scales")
+        place_scales(1)
 
-        pick_words(0, 0, S)
-        for lo, hi in OUT_RANGES[0][:2]:
-            load_res(0, lo, hi)
-        load_w(1, 1, at=AT_LAST_QUARTER)
-        for lo, hi in OUT_RANGES[0][2:]:
-            load_res(0, lo, hi)
-
-        pick_words(1, *PICK_RANGES[0])
+        pick_words(0, *PICK_RANGES[0][0])
         unread = psum.tile([P, BANK], F32, name="unread")
-        for lo in range(0, S, BANK):
+        for n in range(2):
             nc.tensor.matmul_mx(
                 out=unread[:],
                 lhsT=picked_words[0, 0][:, :P].bitcast(FP8X4),
                 lhsT_scale=picked_scales[:, :P],
-                rhs=picked_words[0, 0][:, lo : lo + BANK].bitcast(FP8X4),
-                rhs_scale=picked_scales[:, lo : lo + BANK],
-                start=(lo == 0),
-                stop=(lo + BANK == S),
+                rhs=picked_words[0, 0][:].bitcast(FP8X4),
+                rhs_scale=picked_scales[:, :BANK],
+                start=(n == 0),
+                stop=(n == 1),
             )
-        quantize_w(0, 0, round_w(0, 0))
-        pick_words(1, *PICK_RANGES[1], after="raw00")
-        quantize_w(0, 1, round_w(0, 1))
-        pick_words(1, *PICK_RANGES[2], after="raw01")
-        rounded10 = round_w(1, 0)
-        load_res(1, 0, OUT_RANGES[1][0][1])
-        load_res(1, OUT_RANGES[1][0][1], U)
+        pick_words(0, *PICK_RANGES[0][1])
+        load_res(0, *OUT_RANGES[0][0], at=AT_RES00)
+        load_w(1, 0, at=AT_RAW10)
+        load_res(0, *OUT_RANGES[0][1], at=AT_RES01)
+        load_w(1, 1, at=AT_RAW11)
 
-        y0 = sbuf([P, S], F32, "y0", after="scales")
-        y1 = sbuf([P, S], F32, "y1")
+        quantize_w(0, 0, round_w(0, 0))
         accs0 = accumulators(0)
         for acc, (lo, hi) in zip(accs0, CHUNKS):
             product(acc, 0, 0, lo, hi)
+
+        pick_words(1, *PICK_RANGES[1][0])
+        quantize_w(0, 1, round_w(0, 1))
+        pick_words(1, *PICK_RANGES[1][1], after="scales")
+        load_res(0, *OUT_RANGES[0][2], at=AT_RES02)
+        load_res(0, *OUT_RANGES[0][3], at=AT_RES03)
+        load_res(1, 0, OUT_RANGES[1][0][1], at=AT_RES1)
+        load_res(1, OUT_RANGES[1][0][1], U, at=AT_RES1 + width(1, 0))
+
+        y0 = sbuf([P, S], F32, "y0")
+        y1 = sbuf([P, S], F32, "y1")
         for c, (lo, hi) in enumerate(CHUNKS):
             product(accs0[c], 0, 1, lo, hi)
-            if c < SCALAR_CHUNKS:
-                nc.scalar.activation(y0[:, lo:hi], accs0[c][:], RELU)
-            else:
+            if c in VECTOR_CHUNKS:
                 nc.vector.tensor_scalar_max(y0[:, lo:hi], accs0[c][:], 0.0)
+            else:
+                nc.scalar.activation(y0[:, lo:hi], accs0[c][:], RELU)
 
-        quantize_w(1, 0, rounded10, after="w_codes01")
+        unmerge(0, y0, 0)
+        quantize_w(1, 0, round_w(1, 0, after="w_codes01"))
         accs1 = accumulators(1)
         for acc, (lo, hi) in zip(accs1, CHUNKS):
             product(acc, 1, 0, lo, hi)
-        unmerge(0, y0, 0)
-        unmerge(0, y0, 1)
-        quantize_w(1, 1, round_w(1, 1, at=AT_RES0))
+        unmerge(0, y0, 1, at=AT_SECOND_SUMS)
+        quantize_w(1, 1, round_w(1, 1))
         for acc, (lo, hi) in zip(accs1, CHUNKS):
             product(acc, 1, 1, lo, hi)
             nc.scalar.activation(y1[:, lo:hi], acc[:], RELU)

@@ -32,7 +32,7 @@ CHUNKS = ((0, 256), (256, 512), (512, 768), (768, 896), (896, 1024))
 VECTOR_CHUNKS = (2, 4)
 OUT_RANGES = (
     ((0, 384), (384, 896), (896, 1472), (1472, 2048)),
-    ((0, 960), (960, 1600), (1600, 1920), (1920, 2048)),
+    ((0, 640), (640, 1152), (1152, 1664), (1664, 1920), (1920, 2048)),
 )
 MOVE_ORDER = (0, 2, 1, 3)
 
@@ -155,7 +155,7 @@ def tile_picked_unmerge_relu_p_kernel(tc, x_words, x_scales, w1, res, offs, own,
         for z in range(PASSES):
             nc.vector.memset(placed_scales[z][:].bitcast(I32), 0)
 
-        nc.sync.dma_start(scales[first_row:, :].bitcast(I32), x_scales.rearrange("z r n -> (z r) n").bitcast(I32))
+        nc.scalar.dma_start(scales[first_row:, :].bitcast(I32), x_scales.rearrange("z r n -> (z r) n").bitcast(I32))
         nc.sync.dma_start(offs_sb[:], offs)
         load_words(0)
         load_w(0, 0)
@@ -195,8 +195,8 @@ def tile_picked_unmerge_relu_p_kernel(tc, x_words, x_scales, w1, res, offs, own,
         pick_words(1, *PICK_RANGES[1][1], after="scales")
         load_res(0, *OUT_RANGES[0][2], at=AT_RES02)
         load_res(0, *OUT_RANGES[0][3], at=AT_RES03)
-        load_res(1, 0, OUT_RANGES[1][0][1], at=AT_RES1)
-        load_res(1, OUT_RANGES[1][0][1], U, at=AT_RES1 + width(1, 0))
+        load_res(1, 0, OUT_RANGES[1][1][1], at=AT_RES1)
+        load_res(1, OUT_RANGES[1][1][1], U, at=AT_RES1 + width(1, 0) + width(1, 1))
 
         y0 = sbuf([P, S], F32, "y0")
         y1 = sbuf([P, S], F32, "y1")

@@ -155,7 +155,7 @@ def tile_picked_unmerge_relu_p_kernel(tc, x_words, x_scales, w1, res, offs, own,
         for z in range(PASSES):
             nc.vector.memset(placed_scales[z][:].bitcast(I32), 0)
 
-        nc.scalar.dma_start(scales[first_row:, :].bitcast(I32), x_scales.rearrange("z r n -> (z r) n").bitcast(I32))
+        nc.sync.dma_start(scales[first_row:, :].bitcast(I32), x_scales.rearrange("z r n -> (z r) n").bitcast(I32))
         nc.sync.dma_start(offs_sb[:], offs)
         load_words(0)
         load_w(0, 0)

@@ -23,11 +23,10 @@ QUADRANT = 32
 SCALE_ROWS = K // 32
 ENTRIES_PER_COLUMN = 16
 LINE = 4
-BANK = 512
 WORD_BYTES = 4
 ALIGN = 64
 
-PICK_RANGES = (((0, 512), (512, 1024)), ((0, 768), (768, 1024)))
+PICK_RANGES = ((0, 768), (768, 1024))
 CHUNKS = ((0, 256), (256, 512), (512, 768), (768, 896), (896, 1024))
 VECTOR_CHUNKS = (2, 4)
 OUT_RANGES = (
@@ -167,19 +166,7 @@ def tile_picked_unmerge_relu_p_kernel(tc, x_words, x_scales, w1, res, offs, own,
         load_w(0, 1, after="scales")
         place_scales(1)
 
-        pick_words(0, *PICK_RANGES[0][0])
-        unread = psum.tile([P, BANK], F32, name="unread")
-        for n in range(2):
-            nc.tensor.matmul_mx(
-                out=unread[:],
-                lhsT=picked_words[0, 0][:, :P].bitcast(FP8X4),
-                lhsT_scale=picked_scales[:, :P],
-                rhs=picked_words[0, 0][:].bitcast(FP8X4),
-                rhs_scale=picked_scales[:, :BANK],
-                start=(n == 0),
-                stop=(n == 1),
-            )
-        pick_words(0, *PICK_RANGES[0][1])
+        pick_words(0, 0, S)
         load_res(0, *OUT_RANGES[0][0], at=AT_RES00)
         load_w(1, 0, at=AT_RAW10)
         load_res(0, *OUT_RANGES[0][1], at=AT_RES01)
@@ -190,9 +177,9 @@ def tile_picked_unmerge_relu_p_kernel(tc, x_words, x_scales, w1, res, offs, own,
         for acc, (lo, hi) in zip(accs0, CHUNKS):
             product(acc, 0, 0, lo, hi)
 
-        pick_words(1, *PICK_RANGES[1][0])
+        pick_words(1, *PICK_RANGES[0])
         quantize_w(0, 1, round_w(0, 1))
-        pick_words(1, *PICK_RANGES[1][1], after="scales")
+        pick_words(1, *PICK_RANGES[1], after="scales")
         load_res(0, *OUT_RANGES[0][2], at=AT_RES02)
         load_res(0, *OUT_RANGES[0][3], at=AT_RES03)
         load_res(1, 0, OUT_RANGES[1][1][1], at=AT_RES1)

@@ -27,32 +27,30 @@ WORD_BYTES = 4
 ALIGN = 64
 
 PICK_RANGES = ((0, 768), (768, 1024))
-CHUNKS = ((0, 256), (256, 512), (512, 768), (768, 896), (896, 1024))
-VECTOR_CHUNKS = (2, 4)
-OUT_RANGES = (
-    ((0, 384), (384, 896), (896, 1472), (1472, 2048)),
-    ((0, 640), (640, 1152), (1152, 1664), (1664, 1920), (1920, 2048)),
+CHUNKS = (
+    ((0, 256), (256, 512), (512, 768), (768, 896), (896, 1024)),
+    ((0, 512), (512, 768), (768, 1024)),
 )
+VECTOR_CHUNKS = (4,)
 MOVE_ORDER = (0, 2, 1, 3)
 
-
-def width(b, n):
-    return WORD_BYTES * (OUT_RANGES[b][n][1] - OUT_RANGES[b][n][0])
-
+FUSED = (((0, 512), (1024, 1536)), ((0, 256), (896, 1152), (1664, 1792)))
+SHARED = (((512, 1024), (1536, 2048)), ((256, 896), (1152, 1664), (1792, 2048)))
+RES_RANGES = (((0, 512), (512, 1024), (1024, 2048)), ((0, 1152), (1152, 2048)))
 
 QUARTER = WORD_BYTES * PACK * P
 TABLE = WORD_BYTES * T
-AT_SECOND_SUMS = 0
-AT_RAW10 = AT_SECOND_SUMS + width(0, 1) - ALIGN
-AT_WORDS0 = AT_RAW10 + QUARTER - ALIGN
-AT_RES00 = AT_WORDS0 + ALIGN
-AT_RES01 = AT_RES00 + width(0, 0)
-AT_RAW11 = AT_WORDS0 + TABLE - ALIGN
-AT_THIRD_SUMS = AT_RAW11 + QUARTER - ALIGN
-AT_RES02 = AT_THIRD_SUMS + width(0, 2)
-AT_WORDS1 = AT_RES02 + width(0, 2) - ALIGN
-AT_RES03 = AT_WORDS1 + ALIGN
-AT_RES1 = AT_RES03 + width(0, 3)
+AT_RAW01 = 0
+AT_SCALES = AT_RAW01 + QUARTER - ALIGN
+AT_RAW10 = AT_SCALES + T - ALIGN
+AT_RES10 = AT_RAW10 + QUARTER
+AT_WORDS0 = AT_RES10 + WORD_BYTES * 1152 - ALIGN
+AT_RAW11 = AT_WORDS0 + ALIGN
+AT_RES00 = AT_RAW11 + QUARTER
+AT_RES01 = AT_RES00 + QUARTER
+AT_RES02 = AT_RES01 + QUARTER
+AT_WORDS1 = AT_RES02 + 2 * QUARTER
+AT_RES11 = AT_WORDS1
 
 
 def tile_picked_unmerge_relu_p_kernel(tc, x_words, x_scales, w1, res, offs, own, out):
@@ -62,10 +60,10 @@ def tile_picked_unmerge_relu_p_kernel(tc, x_words, x_scales, w1, res, offs, own,
         laid = ctx.enter_context(tc.tile_pool(name="laid", bufs=1))
         psum = ctx.enter_context(tc.psum_pool(name="psum", bufs=1))
 
-        def sbuf(shape, dtype, name, after=None, at=None):
+        def sbuf(shape, dtype, name, at=None):
             if at is not None:
                 return laid.tile(shape, dtype, name=name, tag=name, align_bytes=ALIGN, offset=at)
-            return keep.tile(shape, dtype, name=name, tag=after or name, align_bytes=ALIGN)
+            return keep.tile(shape, dtype, name=name, tag=name, align_bytes=ALIGN)
 
         def entries(list_tile, lo, hi):
             return list_tile[:, lo // ENTRIES_PER_COLUMN : hi // ENTRIES_PER_COLUMN]
@@ -73,41 +71,49 @@ def tile_picked_unmerge_relu_p_kernel(tc, x_words, x_scales, w1, res, offs, own,
         offs_sb = keep.tile([P, S // ENTRIES_PER_COLUMN], U16, name="offs_sb")
         own_sb = keep.tile([P, U // ENTRIES_PER_COLUMN], U16, name="own_sb")
         words = [sbuf([P, T], I32, "words0", at=AT_WORDS0), sbuf([P, T], I32, "words1", at=AT_WORDS1)]
-        scales = sbuf([P, T], U8, "scales")
+        scales = sbuf([P, T], U8, "scales", at=AT_SCALES)
         picked_scales = sbuf([P, S], U8, "picked_scales")
-        placed_scales = [sbuf([P, S], U8, "placed_scales%d" % z) for z in range(PASSES)]
+        placed_scales = sbuf([P, PASSES * S], U8, "placed_scales")
         w_raw, w_codes, w_scales = {}, {}, {}
         picked_words = {}
         res_sb = {}
+        fetched = {}
         first_row = P - SCALE_ROWS
 
         def load_words(z):
             nc.sync.dma_start(words[z][:], x_words[z].rearrange("p n t -> p (n t)").bitcast(I32))
 
-        def load_w(b, z, after=None, at=None):
-            w_raw[b, z] = sbuf([P, PACK, P], F32, "raw%d%d" % (b, z), after, at)
+        def load_w(b, z, at=None):
+            w_raw[b, z] = sbuf([P, PACK, P], F32, "raw%d%d" % (b, z), at)
             rows = w1[z * P * PACK : (z + 1) * P * PACK, b * P : (b + 1) * P]
             nc.sync.dma_start(w_raw[b, z][:], rows.rearrange("(p t) m -> p t m", t=PACK))
 
-        def load_res(b, lo, hi, at):
+        def load_res(b, n, at):
+            lo, hi = RES_RANGES[b][n]
             res_sb[b, lo] = sbuf([P, hi - lo], F32, "res%d_%d" % (b, lo), at=at)
             nc.sync.dma_start(res_sb[b, lo][:], res[b * P : (b + 1) * P, lo:hi])
 
-        def place_scales(z):
+        def res_columns(b, lo, hi):
+            first = max(start for block, start in res_sb if block == b and start <= lo)
+            return res_sb[b, first][:, lo - first : hi - first]
+
+        def place_scales():
+            rows = PACK * PASSES
             for q in MOVE_ORDER:
-                row = first_row + z * SCALE_ROWS // PASSES + PACK * q
+                row = first_row + rows * q
                 nc.sync.dma_start(
-                    placed_scales[z][QUADRANT * q : QUADRANT * q + PACK, :].bitcast(I32),
-                    picked_scales[row : row + PACK, :].bitcast(I32),
+                    placed_scales[QUADRANT * q : QUADRANT * q + PACK, :].bitcast(I32),
+                    picked_scales[row : row + rows, :].bitcast(I32),
                 )
 
-        def round_w(b, z, after=None):
-            rounded = sbuf([P, P, PACK], BF16, "rounded%d%d" % (b, z), after)
-            nc.scalar.activation(
-                rounded[:].rearrange("p (c i) t -> p c t i", i=LINE),
-                w_raw[b, z][:].rearrange("p t (c i) -> p c t i", i=LINE),
-                COPY,
-            )
+        def round_w(b, z, on_vector=False):
+            rounded = sbuf([P, P, PACK], BF16, "rounded%d%d" % (b, z))
+            dst = rounded[:].rearrange("p (c i) t -> p c t i", i=LINE)
+            src = w_raw[b, z][:].rearrange("p t (c i) -> p c t i", i=LINE)
+            if on_vector:
+                nc.vector.tensor_copy(dst, src)
+            else:
+                nc.scalar.activation(dst, src, COPY)
             return rounded
 
         def quantize_w(b, z, rounded):
@@ -119,12 +125,12 @@ def tile_picked_unmerge_relu_p_kernel(tc, x_words, x_scales, w1, res, offs, own,
                 in_=rounded[:].rearrange("p m t -> p (m t)"),
             )
 
-        def pick_words(z, lo, hi, after=None):
-            picked_words[z, lo] = sbuf([P, hi - lo], U32, "picked_words%d_%d" % (z, lo), after)
+        def pick_words(z, lo, hi, at=None):
+            picked_words[z, lo] = sbuf([P, hi - lo], U32, "picked_words%d_%d" % (z, lo), at)
             nc.vector.tensor_copy(picked_words[z, lo][:], words[z][:].bitcast(U32).indirect(entries(offs_sb, lo, hi)))
 
         def accumulators(b):
-            return [psum.tile([P, hi - lo], F32, name="acc%d_%d" % (b, lo), tag="acc_%d" % lo) for lo, hi in CHUNKS]
+            return [psum.tile([P, hi - lo], F32, name="acc%d_%d" % (b, lo)) for lo, hi in CHUNKS[b]]
 
         def product(acc, b, z, lo, hi):
             first = max(start for pass_of_tile, start in picked_words if pass_of_tile == z and start <= lo)
@@ -133,28 +139,34 @@ def tile_picked_unmerge_relu_p_kernel(tc, x_words, x_scales, w1, res, offs, own,
                 lhsT=w_codes[b, z][:].bitcast(FP8X4),
                 lhsT_scale=w_scales[b, z][:],
                 rhs=picked_words[z, first][:, lo - first : hi - first].bitcast(FP8X4),
-                rhs_scale=placed_scales[z][:, lo:hi],
+                rhs_scale=placed_scales[:, z * S + lo : z * S + hi],
                 start=(z == 0),
                 stop=(z == PASSES - 1),
             )
 
-        def unmerge(b, y, n, at=None):
-            lo, hi = OUT_RANGES[b][n]
-            first = max(start for block, start in res_sb if block == b and start <= lo)
-            sums = sbuf([P, hi - lo], F32, "sums%d_%d" % (b, lo), at=at)
-            nc.vector.tensor_tensor(
-                sums[:],
-                y[:].indirect(entries(own_sb, lo, hi)),
-                res_sb[b, first][:, lo - first : hi - first],
-                ADD,
-            )
+        def store(b, lo, hi, sums):
             nc.sync.dma_start(out[b * P : (b + 1) * P, lo:hi], sums[:])
 
-        nc.vector.memset(scales[:first_row, :].bitcast(I32), 0)
-        for z in range(PASSES):
-            nc.vector.memset(placed_scales[z][:].bitcast(I32), 0)
+        def fetch_and_add(b, n):
+            lo, hi = FUSED[b][n]
+            sums = sbuf([P, hi - lo], F32, "sums%d_%d" % (b, lo))
+            nc.vector.tensor_tensor(sums[:], y[b][:].indirect(entries(own_sb, lo, hi)), res_columns(b, lo, hi), ADD)
+            store(b, lo, hi, sums)
 
-        nc.sync.dma_start(scales[first_row:, :].bitcast(I32), x_scales.rearrange("z r n -> (z r) n").bitcast(I32))
+        def fetch(b, n):
+            lo, hi = SHARED[b][n]
+            fetched[b, n] = sbuf([P, hi - lo], F32, "fetched%d_%d" % (b, lo))
+            nc.scalar.activation(fetched[b, n][:], y[b][:].indirect(entries(own_sb, lo, hi)), COPY)
+
+        def add(b, n):
+            lo, hi = SHARED[b][n]
+            nc.vector.tensor_tensor(fetched[b, n][:], fetched[b, n][:], res_columns(b, lo, hi), ADD)
+            store(b, lo, hi, fetched[b, n])
+
+        nc.vector.memset(scales[:first_row, :].bitcast(I32), 0)
+        nc.vector.memset(placed_scales[:].bitcast(I32), 0)
+
+        nc.sync.dma_start(scales[first_row:, :].bitcast(I32), x_scales.rearrange("z r n -> r z n").bitcast(I32))
         nc.sync.dma_start(offs_sb[:], offs)
         load_words(0)
         load_w(0, 0)
@@ -162,49 +174,55 @@ def tile_picked_unmerge_relu_p_kernel(tc, x_words, x_scales, w1, res, offs, own,
         nc.sync.dma_start(own_sb[:], own)
 
         nc.vector.tensor_copy(picked_scales[:], scales[:].indirect(offs_sb[:]))
-        place_scales(0)
-        load_w(0, 1, after="scales")
-        place_scales(1)
+        place_scales()
+        load_w(0, 1, at=AT_RAW01)
+        load_w(1, 0, at=AT_RAW10)
 
         pick_words(0, 0, S)
-        load_res(0, *OUT_RANGES[0][0], at=AT_RES00)
-        load_w(1, 0, at=AT_RAW10)
-        load_res(0, *OUT_RANGES[0][1], at=AT_RES01)
         load_w(1, 1, at=AT_RAW11)
+        load_res(0, 0, at=AT_RES00)
+        load_res(0, 1, at=AT_RES01)
+        load_res(0, 2, at=AT_RES02)
+        load_res(1, 0, at=AT_RES10)
 
         quantize_w(0, 0, round_w(0, 0))
-        accs0 = accumulators(0)
-        for acc, (lo, hi) in zip(accs0, CHUNKS):
+        accs = [accumulators(b) for b in range(2)]
+        for acc, (lo, hi) in zip(accs[0], CHUNKS[0]):
             product(acc, 0, 0, lo, hi)
 
         pick_words(1, *PICK_RANGES[0])
         quantize_w(0, 1, round_w(0, 1))
-        pick_words(1, *PICK_RANGES[1], after="scales")
-        load_res(0, *OUT_RANGES[0][2], at=AT_RES02)
-        load_res(0, *OUT_RANGES[0][3], at=AT_RES03)
-        load_res(1, 0, OUT_RANGES[1][1][1], at=AT_RES1)
-        load_res(1, OUT_RANGES[1][1][1], U, at=AT_RES1 + width(1, 0) + width(1, 1))
+        pick_words(1, *PICK_RANGES[1], at=AT_RAW01)
+        load_res(1, 1, at=AT_RES11)
+        quantize_w(1, 0, round_w(1, 0))
+        rounded11 = round_w(1, 1, on_vector=True)
 
-        y0 = sbuf([P, S], F32, "y0")
-        y1 = sbuf([P, S], F32, "y1")
-        for c, (lo, hi) in enumerate(CHUNKS):
-            product(accs0[c], 0, 1, lo, hi)
+        y = [sbuf([P, S], F32, "y%d" % b) for b in range(2)]
+        for c, (lo, hi) in enumerate(CHUNKS[0]):
+            product(accs[0][c], 0, 1, lo, hi)
             if c in VECTOR_CHUNKS:
-                nc.vector.tensor_scalar_max(y0[:, lo:hi], accs0[c][:], 0.0)
+                nc.vector.tensor_scalar_max(y[0][:, lo:hi], accs[0][c][:], 0.0)
             else:
-                nc.scalar.activation(y0[:, lo:hi], accs0[c][:], RELU)
+                nc.scalar.activation(y[0][:, lo:hi], accs[0][c][:], RELU)
+        quantize_w(1, 1, rounded11)
 
-        unmerge(0, y0, 0)
-        quantize_w(1, 0, round_w(1, 0, after="w_codes01"))
-        accs1 = accumulators(1)
-        for acc, (lo, hi) in zip(accs1, CHUNKS):
-            product(acc, 1, 0, lo, hi)
-        unmerge(0, y0, 1, at=AT_SECOND_SUMS)
-        quantize_w(1, 1, round_w(1, 1))
-        for acc, (lo, hi) in zip(accs1, CHUNKS):
-            product(acc, 1, 1, lo, hi)
-            nc.scalar.activation(y1[:, lo:hi], acc[:], RELU)
-        unmerge(0, y0, 2, at=AT_THIRD_SUMS)
-        unmerge(0, y0, 3)
-        for n in range(len(OUT_RANGES[1])):
-            unmerge(1, y1, n)
+        fetch(0, 0)
+        fetch_and_add(0, 0)
+        for z in range(PASSES):
+            for acc, (lo, hi) in zip(accs[1], CHUNKS[1]):
+                product(acc, 1, z, lo, hi)
+        for acc, (lo, hi) in zip(accs[1], CHUNKS[1]):
+            nc.scalar.activation(y[1][:, lo:hi], acc[:], RELU)
+        add(0, 0)
+        fetch(0, 1)
+        fetch_and_add(0, 1)
+        fetch(1, 0)
+        fetch_and_add(1, 0)
+        add(0, 1)
+        fetch(1, 1)
+        fetch_and_add(1, 1)
+        add(1, 0)
+        fetch(1, 2)
+        fetch_and_add(1, 2)
+        add(1, 1)
+        add(1, 2)

@@ -34,23 +34,15 @@ CHUNKS = (
 VECTOR_CHUNKS = (4,)
 MOVE_ORDER = (0, 2, 1, 3)
 
-FUSED = (((0, 512), (1024, 1536)), ((0, 256), (896, 1152), (1664, 1792)))
-SHARED = (((512, 1024), (1536, 2048)), ((256, 896), (1152, 1664), (1792, 2048)))
-RES_RANGES = (((0, 512), (512, 1024), (1024, 2048)), ((0, 1152), (1152, 2048)))
+FUSED = (((0, 576), (960, 1600)), ((0, 256), (864, 1056)))
+SHARED = (((576, 960), (1600, 2048)), ((256, 864), (1056, 1600), (1600, 1920), (1920, 2048)))
+STORES = (((0, 960), (960, 2048)), ((0, 864), (864, 1056), (1056, 1600), (1600, 1920), (1920, 2048)))
+RES_RANGES = (((0, 576), (576, 2048)), ((0, 864), (864, 2048)))
 
 QUARTER = WORD_BYTES * PACK * P
-TABLE = WORD_BYTES * T
 AT_RAW01 = 0
 AT_SCALES = AT_RAW01 + QUARTER - ALIGN
-AT_RAW10 = AT_SCALES + T - ALIGN
-AT_RES10 = AT_RAW10 + QUARTER
-AT_WORDS0 = AT_RES10 + WORD_BYTES * 1152 - ALIGN
-AT_RAW11 = AT_WORDS0 + ALIGN
-AT_RES00 = AT_RAW11 + QUARTER
-AT_RES01 = AT_RES00 + QUARTER
-AT_RES02 = AT_RES01 + QUARTER
-AT_WORDS1 = AT_RES02 + 2 * QUARTER
-AT_RES11 = AT_WORDS1
+AT_LATE = AT_SCALES + T - ALIGN
 
 
 def tile_picked_unmerge_relu_p_kernel(tc, x_words, x_scales, w1, res, offs, own, out):
@@ -70,32 +62,29 @@ def tile_picked_unmerge_relu_p_kernel(tc, x_words, x_scales, w1, res, offs, own,
 
         offs_sb = keep.tile([P, S // ENTRIES_PER_COLUMN], U16, name="offs_sb")
         own_sb = keep.tile([P, U // ENTRIES_PER_COLUMN], U16, name="own_sb")
-        words = [sbuf([P, T], I32, "words0", at=AT_WORDS0), sbuf([P, T], I32, "words1", at=AT_WORDS1)]
+        words = [sbuf([P, T], I32, "words%d" % z) for z in range(PASSES)]
         scales = sbuf([P, T], U8, "scales", at=AT_SCALES)
         picked_scales = sbuf([P, S], U8, "picked_scales")
         placed_scales = sbuf([P, PASSES * S], U8, "placed_scales")
         w_raw, w_codes, w_scales = {}, {}, {}
         picked_words = {}
-        res_sb = {}
-        fetched = {}
+        sums = {}
         first_row = P - SCALE_ROWS
 
         def load_words(z):
             nc.sync.dma_start(words[z][:], x_words[z].rearrange("p n t -> p (n t)").bitcast(I32))
 
-        def load_w(b, z, at=None):
-            w_raw[b, z] = sbuf([P, PACK, P], F32, "raw%d%d" % (b, z), at)
+        def load_w(b, z, tile):
+            w_raw[b, z] = tile.rearrange("p (t m) -> p t m", t=PACK)
             rows = w1[z * P * PACK : (z + 1) * P * PACK, b * P : (b + 1) * P]
-            nc.sync.dma_start(w_raw[b, z][:], rows.rearrange("(p t) m -> p t m", t=PACK))
-
-        def load_res(b, n, at):
-            lo, hi = RES_RANGES[b][n]
-            res_sb[b, lo] = sbuf([P, hi - lo], F32, "res%d_%d" % (b, lo), at=at)
-            nc.sync.dma_start(res_sb[b, lo][:], res[b * P : (b + 1) * P, lo:hi])
+            nc.sync.dma_start(w_raw[b, z], rows.rearrange("(p t) m -> p t m", t=PACK))
 
         def res_columns(b, lo, hi):
-            first = max(start for block, start in res_sb if block == b and start <= lo)
-            return res_sb[b, first][:, lo - first : hi - first]
+            first = PASSES * PACK * P + b * U
+            return late[:, first + lo : first + hi]
+
+        def load_res(b, lo, hi):
+            nc.sync.dma_start(res_columns(b, lo, hi), res[b * P : (b + 1) * P, lo:hi])
 
         def place_scales():
             rows = PACK * PASSES
@@ -109,7 +98,7 @@ def tile_picked_unmerge_relu_p_kernel(tc, x_words, x_scales, w1, res, offs, own,
         def round_w(b, z, on_vector=False):
             rounded = sbuf([P, P, PACK], BF16, "rounded%d%d" % (b, z))
             dst = rounded[:].rearrange("p (c i) t -> p c t i", i=LINE)
-            src = w_raw[b, z][:].rearrange("p t (c i) -> p c t i", i=LINE)
+            src = w_raw[b, z].rearrange("p t (c i) -> p c t i", i=LINE)
             if on_vector:
                 nc.vector.tensor_copy(dst, src)
             else:
@@ -144,24 +133,31 @@ def tile_picked_unmerge_relu_p_kernel(tc, x_words, x_scales, w1, res, offs, own,
                 stop=(z == PASSES - 1),
             )
 
-        def store(b, lo, hi, sums):
-            nc.sync.dma_start(out[b * P : (b + 1) * P, lo:hi], sums[:])
+        def sums_columns(b, lo, hi):
+            first, last = [(start, stop) for start, stop in STORES[b] if start <= lo < stop][0]
+            if (b, first) not in sums:
+                sums[b, first] = sbuf([P, last - first], F32, "sums%d_%d" % (b, first))
+            return sums[b, first][:, lo - first : hi - first]
+
+        def store_if_whole(b, hi):
+            for first, last in STORES[b]:
+                if last == hi:
+                    nc.sync.dma_start(out[b * P : (b + 1) * P, first:last], sums[b, first][:])
 
         def fetch_and_add(b, n):
             lo, hi = FUSED[b][n]
-            sums = sbuf([P, hi - lo], F32, "sums%d_%d" % (b, lo))
-            nc.vector.tensor_tensor(sums[:], y[b][:].indirect(entries(own_sb, lo, hi)), res_columns(b, lo, hi), ADD)
-            store(b, lo, hi, sums)
+            picked_y = y[b][:].indirect(entries(own_sb, lo, hi))
+            nc.vector.tensor_tensor(sums_columns(b, lo, hi), picked_y, res_columns(b, lo, hi), ADD)
+            store_if_whole(b, hi)
 
         def fetch(b, n):
             lo, hi = SHARED[b][n]
-            fetched[b, n] = sbuf([P, hi - lo], F32, "fetched%d_%d" % (b, lo))
-            nc.scalar.activation(fetched[b, n][:], y[b][:].indirect(entries(own_sb, lo, hi)), COPY)
+            nc.scalar.activation(sums_columns(b, lo, hi), y[b][:].indirect(entries(own_sb, lo, hi)), COPY)
 
         def add(b, n):
             lo, hi = SHARED[b][n]
-            nc.vector.tensor_tensor(fetched[b, n][:], fetched[b, n][:], res_columns(b, lo, hi), ADD)
-            store(b, lo, hi, fetched[b, n])
+            nc.vector.tensor_tensor(sums_columns(b, lo, hi), sums_columns(b, lo, hi), res_columns(b, lo, hi), ADD)
+            store_if_whole(b, hi)
 
         nc.vector.memset(scales[:first_row, :].bitcast(I32), 0)
         nc.vector.memset(placed_scales[:].bitcast(I32), 0)
@@ -169,22 +165,21 @@ def tile_picked_unmerge_relu_p_kernel(tc, x_words, x_scales, w1, res, offs, own,
         nc.sync.dma_start(scales[first_row:, :].bitcast(I32), x_scales.rearrange("z r n -> r z n").bitcast(I32))
         nc.sync.dma_start(offs_sb[:], offs)
         load_words(0)
-        load_w(0, 0)
-        load_words(1)
+        load_w(0, 0, sbuf([P, PACK * P], F32, "raw00")[:])
         nc.sync.dma_start(own_sb[:], own)
+        load_words(1)
 
         nc.vector.tensor_copy(picked_scales[:], scales[:].indirect(offs_sb[:]))
         place_scales()
-        load_w(0, 1, at=AT_RAW01)
-        load_w(1, 0, at=AT_RAW10)
+        load_w(0, 1, sbuf([P, PACK * P], F32, "raw01", at=AT_RAW01)[:])
+        late = sbuf([P, PASSES * PACK * P + N // P * U], F32, "late", at=AT_LATE)
+        for z in range(PASSES):
+            load_w(1, z, late[:, z * PACK * P : (z + 1) * PACK * P])
+        for b in range(N // P):
+            for lo, hi in RES_RANGES[b]:
+                load_res(b, lo, hi)
 
         pick_words(0, 0, S)
-        load_w(1, 1, at=AT_RAW11)
-        load_res(0, 0, at=AT_RES00)
-        load_res(0, 1, at=AT_RES01)
-        load_res(0, 2, at=AT_RES02)
-        load_res(1, 0, at=AT_RES10)
-
         quantize_w(0, 0, round_w(0, 0))
         accs = [accumulators(b) for b in range(2)]
         for acc, (lo, hi) in zip(accs[0], CHUNKS[0]):
@@ -193,7 +188,6 @@ def tile_picked_unmerge_relu_p_kernel(tc, x_words, x_scales, w1, res, offs, own,
         pick_words(1, *PICK_RANGES[0])
         quantize_w(0, 1, round_w(0, 1))
         pick_words(1, *PICK_RANGES[1], at=AT_RAW01)
-        load_res(1, 1, at=AT_RES11)
         quantize_w(1, 0, round_w(1, 0))
         rounded11 = round_w(1, 1, on_vector=True)
 
@@ -217,12 +211,13 @@ def tile_picked_unmerge_relu_p_kernel(tc, x_words, x_scales, w1, res, offs, own,
         fetch(0, 1)
         fetch_and_add(0, 1)
         fetch(1, 0)
-        fetch_and_add(1, 0)
         add(0, 1)
+        fetch_and_add(1, 0)
         fetch(1, 1)
-        fetch_and_add(1, 1)
         add(1, 0)
+        fetch_and_add(1, 1)
         fetch(1, 2)
-        fetch_and_add(1, 2)
         add(1, 1)
+        fetch(1, 3)
         add(1, 2)
+        add(1, 3)

@@ -34,9 +34,9 @@ CHUNKS = (
 VECTOR_CHUNKS = (4,)
 MOVE_ORDER = (0, 2, 1, 3)
 
-FUSED = (((0, 576), (960, 1600)), ((0, 256), (864, 1056)))
-SHARED = (((576, 960), (1600, 2048)), ((256, 864), (1056, 1600), (1600, 1920), (1920, 2048)))
-STORES = (((0, 960), (960, 2048)), ((0, 864), (864, 1056), (1056, 1600), (1600, 1920), (1920, 2048)))
+FUSED = (((0, 576), (960, 1600)), ((0, 352), (864, 1152)))
+SHARED = (((576, 960), (1600, 2048)), ((352, 864), (1152, 1600), (1600, 1920), (1920, 2048)))
+STORES = (((0, 960), (960, 2048)), ((0, 864), (864, 1152), (1152, 1600), (1600, 1920), (1920, 2048)))
 RES_RANGES = (((0, 576), (576, 2048)), ((0, 864), (864, 2048)))
 
 QUARTER = WORD_BYTES * PACK * P

@@ -34,10 +34,10 @@ CHUNKS = (
 VECTOR_CHUNKS = (4,)
 MOVE_ORDER = (0, 2, 1, 3)
 
-FUSED = (((0, 576), (960, 1600)), ((0, 352), (864, 1152)))
-SHARED = (((576, 960), (1600, 2048)), ((352, 864), (1152, 1600), (1600, 1920), (1920, 2048)))
-STORES = (((0, 960), (960, 2048)), ((0, 864), (864, 1152), (1152, 1600), (1600, 1920), (1920, 2048)))
-RES_RANGES = (((0, 576), (576, 2048)), ((0, 864), (864, 2048)))
+FUSED = (((0, 576), (960, 1600)), ((0, 320), (832, 1088), (1504, 1664)))
+SHARED = (((576, 960), (1600, 2048)), ((320, 832), (1088, 1504), (1664, 1920), (1920, 2048)))
+STORES = (((0, 960), (960, 2048)), ((0, 832), (832, 1088), (1088, 1504), (1504, 1664), (1664, 1920), (1920, 2048)))
+RES_RANGES = (((0, 576), (576, 2048)), ((0, 2048),))
 
 QUARTER = WORD_BYTES * PACK * P
 AT_RAW01 = 0
@@ -218,6 +218,7 @@ def tile_picked_unmerge_relu_p_kernel(tc, x_words, x_scales, w1, res, offs, own,
         fetch_and_add(1, 1)
         fetch(1, 2)
         add(1, 1)
+        fetch_and_add(1, 2)
         fetch(1, 3)
         add(1, 2)
         add(1, 3)

@@ -31,16 +31,18 @@ CHUNKS = (
     ((0, 256), (256, 512), (512, 768), (768, 896), (896, 1024)),
     ((0, 512), (512, 768), (768, 1024)),
 )
-VECTOR_CHUNKS = (4,)
+BANKS = ((0, 1, 2, 3, 4), (5, 0, 1))
+VECTOR_CHUNKS = (2, 4)
 MOVE_ORDER = (0, 2, 1, 3)
 
-FUSED = (((0, 576), (960, 1600)), ((0, 320), (832, 1088), (1504, 1664)))
-SHARED = (((576, 960), (1600, 2048)), ((320, 832), (1088, 1504), (1664, 1920), (1920, 2048)))
-STORES = (((0, 960), (960, 2048)), ((0, 832), (832, 1088), (1088, 1504), (1504, 1664), (1664, 1920), (1920, 2048)))
+FUSED = (((0, 576), (960, 1600)), ((0, 416), (1056, 1280)))
+SHARED = (((576, 960), (1600, 2048)), ((416, 1056), (1280, 1664), (1664, 1920), (1920, 2048)))
+STORES = (((0, 960), (960, 1600), (1600, 2048)), ((0, 416), (416, 1056), (1056, 1280), (1280, 1664), (1664, 1920), (1920, 2048)))
 RES_RANGES = (((0, 576), (576, 2048)), ((0, 2048),))
 
 QUARTER = WORD_BYTES * PACK * P
-AT_RAW01 = 0
+AT_RAW0 = 0
+AT_RAW01 = AT_RAW0 + 2 * QUARTER
 AT_SCALES = AT_RAW01 + QUARTER - ALIGN
 AT_LATE = AT_SCALES + T - ALIGN
 
@@ -74,13 +76,13 @@ def tile_picked_unmerge_relu_p_kernel(tc, x_words, x_scales, w1, res, offs, own,
         def load_words(z):
             nc.sync.dma_start(words[z][:], x_words[z].rearrange("p n t -> p (n t)").bitcast(I32))
 
-        def load_w(b, z, tile):
-            w_raw[b, z] = tile.rearrange("p (t m) -> p t m", t=PACK)
-            rows = w1[z * P * PACK : (z + 1) * P * PACK, b * P : (b + 1) * P]
-            nc.sync.dma_start(w_raw[b, z], rows.rearrange("(p t) m -> p t m", t=PACK))
+        def load_w(z, blocks, tile):
+            w_raw[z, blocks[0]] = tile.rearrange("p (t m) -> p t m", t=PACK)
+            rows = w1[z * P * PACK : (z + 1) * P * PACK, blocks[0] * P : (blocks[-1] + 1) * P]
+            nc.sync.dma_start(w_raw[z, blocks[0]], rows.rearrange("(p t) m -> p t m", t=PACK))
 
         def res_columns(b, lo, hi):
-            first = PASSES * PACK * P + b * U
+            first = PACK * P + b * U
             return late[:, first + lo : first + hi]
 
         def load_res(b, lo, hi):
@@ -95,38 +97,36 @@ def tile_picked_unmerge_relu_p_kernel(tc, x_words, x_scales, w1, res, offs, own,
                     picked_scales[row : row + rows, :].bitcast(I32),
                 )
 
-        def round_w(b, z, on_vector=False):
-            rounded = sbuf([P, P, PACK], BF16, "rounded%d%d" % (b, z))
-            dst = rounded[:].rearrange("p (c i) t -> p c t i", i=LINE)
-            src = w_raw[b, z].rearrange("p t (c i) -> p c t i", i=LINE)
-            if on_vector:
-                nc.vector.tensor_copy(dst, src)
-            else:
-                nc.scalar.activation(dst, src, COPY)
+        def round_w(z, blocks):
+            rounded = sbuf([P, PACK * P * len(blocks)], BF16, "rounded%d%d" % (z, blocks[0]))
+            nc.scalar.activation(
+                rounded[:].rearrange("p (c i t) -> p c t i", i=LINE, t=PACK),
+                w_raw[z, blocks[0]].rearrange("p t (c i) -> p c t i", i=LINE),
+                COPY,
+            )
             return rounded
 
-        def quantize_w(b, z, rounded):
-            w_codes[b, z] = sbuf([P, P], U32, "w_codes%d%d" % (b, z))
-            w_scales[b, z] = sbuf([P, P], U8, "w_scales%d%d" % (b, z))
-            nc.vector.quantize_mx(
-                out=w_codes[b, z][:].bitcast(FP8X4),
-                scales=w_scales[b, z][:],
-                in_=rounded[:].rearrange("p m t -> p (m t)"),
-            )
+        def quantize_w(z, blocks, rounded):
+            codes = sbuf([P, P * len(blocks)], U32, "w_codes%d%d" % (z, blocks[0]))
+            planes = sbuf([P, P * len(blocks)], U8, "w_scales%d%d" % (z, blocks[0]))
+            nc.vector.quantize_mx(out=codes[:].bitcast(FP8X4), scales=planes[:], in_=rounded[:])
+            for n, b in enumerate(blocks):
+                w_codes[b, z] = codes[:, n * P : (n + 1) * P]
+                w_scales[b, z] = planes[:, n * P : (n + 1) * P]
 
         def pick_words(z, lo, hi, at=None):
             picked_words[z, lo] = sbuf([P, hi - lo], U32, "picked_words%d_%d" % (z, lo), at)
             nc.vector.tensor_copy(picked_words[z, lo][:], words[z][:].bitcast(U32).indirect(entries(offs_sb, lo, hi)))
 
         def accumulators(b):
-            return [psum.tile([P, hi - lo], F32, name="acc%d_%d" % (b, lo)) for lo, hi in CHUNKS[b]]
+            return [psum.tile([P, hi - lo], F32, name="acc%d_%d" % (b, lo), tag="bank%d" % BANKS[b][c]) for c, (lo, hi) in enumerate(CHUNKS[b])]
 
         def product(acc, b, z, lo, hi):
             first = max(start for pass_of_tile, start in picked_words if pass_of_tile == z and start <= lo)
             nc.tensor.matmul_mx(
                 out=acc[:],
-                lhsT=w_codes[b, z][:].bitcast(FP8X4),
-                lhsT_scale=w_scales[b, z][:],
+                lhsT=w_codes[b, z].bitcast(FP8X4),
+                lhsT_scale=w_scales[b, z],
                 rhs=picked_words[z, first][:, lo - first : hi - first].bitcast(FP8X4),
                 rhs_scale=placed_scales[:, z * S + lo : z * S + hi],
                 start=(z == 0),
@@ -165,46 +165,45 @@ def tile_picked_unmerge_relu_p_kernel(tc, x_words, x_scales, w1, res, offs, own,
         nc.sync.dma_start(scales[first_row:, :].bitcast(I32), x_scales.rearrange("z r n -> r z n").bitcast(I32))
         nc.sync.dma_start(offs_sb[:], offs)
         load_words(0)
-        load_w(0, 0, sbuf([P, PACK * P], F32, "raw00")[:])
-        nc.sync.dma_start(own_sb[:], own)
+        load_w(0, (0, 1), sbuf([P, PACK * N], F32, "raw0", at=AT_RAW0)[:])
         load_words(1)
+        nc.sync.dma_start(own_sb[:], own)
 
         nc.vector.tensor_copy(picked_scales[:], scales[:].indirect(offs_sb[:]))
         place_scales()
-        load_w(0, 1, sbuf([P, PACK * P], F32, "raw01", at=AT_RAW01)[:])
-        late = sbuf([P, PASSES * PACK * P + N // P * U], F32, "late", at=AT_LATE)
-        for z in range(PASSES):
-            load_w(1, z, late[:, z * PACK * P : (z + 1) * PACK * P])
+        load_w(1, (0,), sbuf([P, PACK * P], F32, "raw10", at=AT_RAW01)[:])
+        late = sbuf([P, PACK * P + N // P * U], F32, "late", at=AT_LATE)
+        load_w(1, (1,), late[:, : PACK * P])
         for b in range(N // P):
             for lo, hi in RES_RANGES[b]:
                 load_res(b, lo, hi)
 
         pick_words(0, 0, S)
-        quantize_w(0, 0, round_w(0, 0))
-        accs = [accumulators(b) for b in range(2)]
+        quantize_w(0, (0, 1), round_w(0, (0, 1)))
+        accs = [accumulators(0)]
         for acc, (lo, hi) in zip(accs[0], CHUNKS[0]):
             product(acc, 0, 0, lo, hi)
 
-        pick_words(1, *PICK_RANGES[0])
-        quantize_w(0, 1, round_w(0, 1))
+        pick_words(1, *PICK_RANGES[0], at=AT_RAW0)
+        quantize_w(1, (0,), round_w(1, (0,)))
         pick_words(1, *PICK_RANGES[1], at=AT_RAW01)
-        quantize_w(1, 0, round_w(1, 0))
-        rounded11 = round_w(1, 1, on_vector=True)
+        quantize_w(1, (1,), round_w(1, (1,)))
 
-        y = [sbuf([P, S], F32, "y%d" % b) for b in range(2)]
+        y = [sbuf([P, S], F32, "y0")]
         for c, (lo, hi) in enumerate(CHUNKS[0]):
             product(accs[0][c], 0, 1, lo, hi)
             if c in VECTOR_CHUNKS:
                 nc.vector.tensor_scalar_max(y[0][:, lo:hi], accs[0][c][:], 0.0)
             else:
                 nc.scalar.activation(y[0][:, lo:hi], accs[0][c][:], RELU)
-        quantize_w(1, 1, rounded11)
 
         fetch(0, 0)
         fetch_and_add(0, 0)
+        accs.append(accumulators(1))
         for z in range(PASSES):
             for acc, (lo, hi) in zip(accs[1], CHUNKS[1]):
                 product(acc, 1, z, lo, hi)
+        y.append(sbuf([P, S], F32, "y1", at=AT_RAW0))
         for acc, (lo, hi) in zip(accs[1], CHUNKS[1]):
             nc.scalar.activation(y[1][:, lo:hi], acc[:], RELU)
         add(0, 0)
@@ -218,7 +217,6 @@ def tile_picked_unmerge_relu_p_kernel(tc, x_words, x_scales, w1, res, offs, own,
         fetch_and_add(1, 1)
         fetch(1, 2)
         add(1, 1)
-        fetch_and_add(1, 2)
         fetch(1, 3)
         add(1, 2)
         add(1, 3)

@@ -26,13 +26,13 @@ LINE = 4
 WORD_BYTES = 4
 ALIGN = 64
 
-PICK_RANGES = ((0, 768), (768, 1024))
+PICK_RANGES = ((0, 896), (896, 1024))
 CHUNKS = (
     ((0, 256), (256, 512), (512, 768), (768, 896), (896, 1024)),
     ((0, 512), (512, 768), (768, 1024)),
 )
 BANKS = ((0, 1, 2, 3, 4), (5, 0, 1))
-VECTOR_CHUNKS = (2, 4)
+VECTOR_CHUNKS = (1, 3)
 MOVE_ORDER = (0, 2, 1, 3)
 
 FUSED = (((0, 576), (960, 1600)), ((0, 416), (1056, 1280)))
@@ -124,7 +124,7 @@ def tile_picked_unmerge_relu_p_kernel(tc, x_words, x_scales, w1, res, offs, own,
         def product(acc, b, z, lo, hi):
             first = max(start for pass_of_tile, start in picked_words if pass_of_tile == z and start <= lo)
             nc.tensor.matmul_mx(
-                out=acc[:],
+                out=acc,
                 lhsT=w_codes[b, z].bitcast(FP8X4),
                 lhsT_scale=w_scales[b, z],
                 rhs=picked_words[z, first][:, lo - first : hi - first].bitcast(FP8X4),
@@ -182,7 +182,7 @@ def tile_picked_unmerge_relu_p_kernel(tc, x_words, x_scales, w1, res, offs, own,
         quantize_w(0, (0, 1), round_w(0, (0, 1)))
         accs = [accumulators(0)]
         for acc, (lo, hi) in zip(accs[0], CHUNKS[0]):
-            product(acc, 0, 0, lo, hi)
+            product(acc[:], 0, 0, lo, hi)
 
         pick_words(1, *PICK_RANGES[0], at=AT_RAW0)
         quantize_w(1, (0,), round_w(1, (0,)))
@@ -191,7 +191,7 @@ def tile_picked_unmerge_relu_p_kernel(tc, x_words, x_scales, w1, res, offs, own,
 
         y = [sbuf([P, S], F32, "y0")]
         for c, (lo, hi) in enumerate(CHUNKS[0]):
-            product(accs[0][c], 0, 1, lo, hi)
+            product(accs[0][c][:], 0, 1, lo, hi)
             if c in VECTOR_CHUNKS:
                 nc.vector.tensor_scalar_max(y[0][:, lo:hi], accs[0][c][:], 0.0)
             else:
@@ -200,9 +200,11 @@ def tile_picked_unmerge_relu_p_kernel(tc, x_words, x_scales, w1, res, offs, own,
         fetch(0, 0)
         fetch_and_add(0, 0)
         accs.append(accumulators(1))
-        for z in range(PASSES):
-            for acc, (lo, hi) in zip(accs[1], CHUNKS[1]):
-                product(acc, 1, z, lo, hi)
+        for acc, (first, last) in zip(accs[1], CHUNKS[1]):
+            borders = [first] + [lo for lo, hi in PICK_RANGES if first < lo < last] + [last]
+            for lo, hi in zip(borders, borders[1:]):
+                for z in range(PASSES):
+                    product(acc[:, lo - first : hi - first], 1, z, lo, hi)
         y.append(sbuf([P, S], F32, "y1", at=AT_RAW0))
         for acc, (lo, hi) in zip(accs[1], CHUNKS[1]):
             nc.scalar.activation(y[1][:, lo:hi], acc[:], RELU)

@@ -29,9 +29,9 @@ ALIGN = 64
 PICK_RANGES = ((0, 896), (896, 1024))
 CHUNKS = (
     ((0, 256), (256, 512), (512, 768), (768, 896), (896, 1024)),
-    ((0, 512), (512, 768), (768, 1024)),
+    ((0, 256), (256, 768), (768, 1024)),
 )
-BANKS = ((0, 1, 2, 3, 4), (5, 0, 1))
+BANKS = ((0, 1, 2, 3, 4), (5, 6, 7))
 VECTOR_CHUNKS = (1, 3)
 MOVE_ORDER = (0, 2, 1, 3)
 
@@ -121,7 +121,7 @@ def tile_picked_unmerge_relu_p_kernel(tc, x_words, x_scales, w1, res, offs, own,
         def accumulators(b):
             return [psum.tile([P, hi - lo], F32, name="acc%d_%d" % (b, lo), tag="bank%d" % BANKS[b][c]) for c, (lo, hi) in enumerate(CHUNKS[b])]
 
-        def product(acc, b, z, lo, hi):
+        def product(acc, b, z, lo, hi, opening=0):
             first = max(start for pass_of_tile, start in picked_words if pass_of_tile == z and start <= lo)
             nc.tensor.matmul_mx(
                 out=acc,
@@ -129,8 +129,8 @@ def tile_picked_unmerge_relu_p_kernel(tc, x_words, x_scales, w1, res, offs, own,
                 lhsT_scale=w_scales[b, z],
                 rhs=picked_words[z, first][:, lo - first : hi - first].bitcast(FP8X4),
                 rhs_scale=placed_scales[:, z * S + lo : z * S + hi],
-                start=(z == 0),
-                stop=(z == PASSES - 1),
+                start=(z == opening),
+                stop=(z != opening),
             )
 
         def sums_columns(b, lo, hi):
@@ -203,8 +203,9 @@ def tile_picked_unmerge_relu_p_kernel(tc, x_words, x_scales, w1, res, offs, own,
         for acc, (first, last) in zip(accs[1], CHUNKS[1]):
             borders = [first] + [lo for lo, hi in PICK_RANGES if first < lo < last] + [last]
             for lo, hi in zip(borders, borders[1:]):
-                for z in range(PASSES):
-                    product(acc[:, lo - first : hi - first], 1, z, lo, hi)
+                opening = 0 if first == 0 else 1
+                for z in (opening, 1 - opening):
+                    product(acc[:, lo - first : hi - first], 1, z, lo, hi, opening)
         y.append(sbuf([P, S], F32, "y1", at=AT_RAW0))
         for acc, (lo, hi) in zip(accs[1], CHUNKS[1]):
             nc.scalar.activation(y[1][:, lo:hi], acc[:], RELU)

@@ -25,25 +25,27 @@ ENTRIES_PER_COLUMN = 16
 LINE = 4
 WORD_BYTES = 4
 ALIGN = 64
+MOVE_ORDER = (0, 2, 1, 3)
 
-PICK_RANGES = ((0, 896), (896, 1024))
+PICK_RANGES = ((0, 512), (512, 896), (896, 1024))
 CHUNKS = (
     ((0, 256), (256, 512), (512, 768), (768, 896), (896, 1024)),
-    ((0, 256), (256, 768), (768, 1024)),
+    ((0, 512), (512, 1024)),
 )
-BANKS = ((0, 1, 2, 3, 4), (5, 6, 7))
 VECTOR_CHUNKS = (1, 3)
-MOVE_ORDER = (0, 2, 1, 3)
+BANKS = ((0, 1, 2, 3, 4), (5, 6))
 
 FUSED = (((0, 576), (960, 1600)), ((0, 416), (1056, 1280)))
 SHARED = (((576, 960), (1600, 2048)), ((416, 1056), (1280, 1664), (1664, 1920), (1920, 2048)))
-STORES = (((0, 960), (960, 1600), (1600, 2048)), ((0, 416), (416, 1056), (1056, 1280), (1280, 1664), (1664, 1920), (1920, 2048)))
+STORES = (((0, 960), (960, 2048)), ((0, 416), (416, 1056), (1056, 1280), (1280, 1664), (1664, 1920), (1920, 2048)))
 RES_RANGES = (((0, 576), (576, 2048)), ((0, 2048),))
+SUMS_AT = {}
 
-QUARTER = WORD_BYTES * PACK * P
-AT_RAW0 = 0
-AT_RAW01 = AT_RAW0 + 2 * QUARTER
-AT_SCALES = AT_RAW01 + QUARTER - ALIGN
+QUARTER = PACK * P
+LATE_WEIGHTS = 3 * QUARTER
+AT_ROUNDED00 = 0
+AT_ROUNDED10 = AT_ROUNDED00 + 4 * QUARTER
+AT_SCALES = AT_ROUNDED10 + 2 * QUARTER
 AT_LATE = AT_SCALES + T - ALIGN
 
 
@@ -77,12 +79,14 @@ def tile_picked_unmerge_relu_p_kernel(tc, x_words, x_scales, w1, res, offs, own,
             nc.sync.dma_start(words[z][:], x_words[z].rearrange("p n t -> p (n t)").bitcast(I32))
 
         def load_w(z, blocks, tile):
-            w_raw[z, blocks[0]] = tile.rearrange("p (t m) -> p t m", t=PACK)
+            whole = tile.rearrange("p (t m) -> p t m", t=PACK)
+            for n, b in enumerate(blocks):
+                w_raw[z, b] = whole[:, :, n * P : (n + 1) * P]
             rows = w1[z * P * PACK : (z + 1) * P * PACK, blocks[0] * P : (blocks[-1] + 1) * P]
-            nc.sync.dma_start(w_raw[z, blocks[0]], rows.rearrange("(p t) m -> p t m", t=PACK))
+            nc.sync.dma_start(whole, rows.rearrange("(p t) m -> p t m", t=PACK))
 
         def res_columns(b, lo, hi):
-            first = PACK * P + b * U
+            first = LATE_WEIGHTS + b * U
             return late[:, first + lo : first + hi]
 
         def load_res(b, lo, hi):
@@ -97,22 +101,22 @@ def tile_picked_unmerge_relu_p_kernel(tc, x_words, x_scales, w1, res, offs, own,
                     picked_scales[row : row + rows, :].bitcast(I32),
                 )
 
-        def round_w(z, blocks):
-            rounded = sbuf([P, PACK * P * len(blocks)], BF16, "rounded%d%d" % (z, blocks[0]))
-            nc.scalar.activation(
-                rounded[:].rearrange("p (c i t) -> p c t i", i=LINE, t=PACK),
-                w_raw[z, blocks[0]].rearrange("p t (c i) -> p c t i", i=LINE),
-                COPY,
-            )
-            return rounded
+        def round_w(engine, z, b, rounded, lo=0, hi=P):
+            target = rounded[:, PACK * lo : PACK * hi].rearrange("p (c i t) -> p c t i", i=LINE, t=PACK)
+            source = w_raw[z, b][:, :, lo:hi].rearrange("p t (c i) -> p c t i", i=LINE)
+            if engine is nc.scalar:
+                nc.scalar.activation(target, source, COPY)
+            else:
+                engine.tensor_copy(target, source)
 
-        def quantize_w(z, blocks, rounded):
-            codes = sbuf([P, P * len(blocks)], U32, "w_codes%d%d" % (z, blocks[0]))
-            planes = sbuf([P, P * len(blocks)], U8, "w_scales%d%d" % (z, blocks[0]))
+        def quantize_w(quarters, rounded):
+            name = "".join(["%d%d" % quarter for quarter in quarters])
+            codes = sbuf([P, P * len(quarters)], U32, "w_codes" + name)
+            planes = sbuf([P, P * len(quarters)], U8, "w_scales" + name)
             nc.vector.quantize_mx(out=codes[:].bitcast(FP8X4), scales=planes[:], in_=rounded[:])
-            for n, b in enumerate(blocks):
-                w_codes[b, z] = codes[:, n * P : (n + 1) * P]
-                w_scales[b, z] = planes[:, n * P : (n + 1) * P]
+            for n, quarter in enumerate(quarters):
+                w_codes[quarter] = codes[:, n * P : (n + 1) * P]
+                w_scales[quarter] = planes[:, n * P : (n + 1) * P]
 
         def pick_words(z, lo, hi, at=None):
             picked_words[z, lo] = sbuf([P, hi - lo], U32, "picked_words%d_%d" % (z, lo), at)
@@ -125,18 +129,24 @@ def tile_picked_unmerge_relu_p_kernel(tc, x_words, x_scales, w1, res, offs, own,
             first = max(start for pass_of_tile, start in picked_words if pass_of_tile == z and start <= lo)
             nc.tensor.matmul_mx(
                 out=acc,
-                lhsT=w_codes[b, z].bitcast(FP8X4),
-                lhsT_scale=w_scales[b, z],
+                lhsT=w_codes[z, b].bitcast(FP8X4),
+                lhsT_scale=w_scales[z, b],
                 rhs=picked_words[z, first][:, lo - first : hi - first].bitcast(FP8X4),
                 rhs_scale=placed_scales[:, z * S + lo : z * S + hi],
                 start=(z == opening),
                 stop=(z != opening),
             )
 
+        def relu(engine, b, acc, lo, hi):
+            if engine is nc.scalar:
+                nc.scalar.activation(y[b][:, lo:hi], acc, RELU)
+            else:
+                nc.vector.tensor_scalar_max(y[b][:, lo:hi], acc, 0.0)
+
         def sums_columns(b, lo, hi):
             first, last = [(start, stop) for start, stop in STORES[b] if start <= lo < stop][0]
             if (b, first) not in sums:
-                sums[b, first] = sbuf([P, last - first], F32, "sums%d_%d" % (b, first))
+                sums[b, first] = sbuf([P, last - first], F32, "sums%d_%d" % (b, first), SUMS_AT.get((b, first)))
             return sums[b, first][:, lo - first : hi - first]
 
         def store_if_whole(b, hi):
@@ -164,51 +174,53 @@ def tile_picked_unmerge_relu_p_kernel(tc, x_words, x_scales, w1, res, offs, own,
 
         nc.sync.dma_start(scales[first_row:, :].bitcast(I32), x_scales.rearrange("z r n -> r z n").bitcast(I32))
         nc.sync.dma_start(offs_sb[:], offs)
-        load_words(0)
-        load_w(0, (0, 1), sbuf([P, PACK * N], F32, "raw0", at=AT_RAW0)[:])
-        load_words(1)
         nc.sync.dma_start(own_sb[:], own)
+        load_words(0)
+        load_words(1)
+        load_w(0, (0,), sbuf([P, QUARTER], F32, "raw00")[:])
 
         nc.vector.tensor_copy(picked_scales[:], scales[:].indirect(offs_sb[:]))
         place_scales()
-        load_w(1, (0,), sbuf([P, PACK * P], F32, "raw10", at=AT_RAW01)[:])
-        late = sbuf([P, PACK * P + N // P * U], F32, "late", at=AT_LATE)
-        load_w(1, (1,), late[:, : PACK * P])
+        late = sbuf([P, LATE_WEIGHTS + N // P * U], F32, "late", at=AT_LATE)
+        for n, (z, b) in enumerate(((1, 0), (0, 1), (1, 1))):
+            load_w(z, (b,), late[:, n * QUARTER : (n + 1) * QUARTER])
         for b in range(N // P):
             for lo, hi in RES_RANGES[b]:
                 load_res(b, lo, hi)
 
         pick_words(0, 0, S)
-        quantize_w(0, (0, 1), round_w(0, (0, 1)))
+        pick_words(1, *PICK_RANGES[0])
+        rounded00 = sbuf([P, QUARTER], BF16, "rounded00", at=AT_ROUNDED00)
+        round_w(nc.scalar, 0, 0, rounded00)
+        quantize_w(((0, 0),), rounded00)
         accs = [accumulators(0)]
         for acc, (lo, hi) in zip(accs[0], CHUNKS[0]):
             product(acc[:], 0, 0, lo, hi)
+        pick_words(1, *PICK_RANGES[1], at=AT_ROUNDED00)
+        rounded10 = sbuf([P, QUARTER], BF16, "rounded10", at=AT_ROUNDED10)
+        round_w(nc.scalar, 1, 0, rounded10)
+        quantize_w(((1, 0),), rounded10)
+        pick_words(1, *PICK_RANGES[2], at=AT_ROUNDED10)
+        rounded_late = sbuf([P, 2 * QUARTER], BF16, "rounded_late")
+        round_w(nc.scalar, 0, 1, rounded_late[:, :QUARTER])
+        round_w(nc.scalar, 1, 1, rounded_late[:, QUARTER:])
+        quantize_w(((0, 1), (1, 1)), rounded_late)
 
-        pick_words(1, *PICK_RANGES[0], at=AT_RAW0)
-        quantize_w(1, (0,), round_w(1, (0,)))
-        pick_words(1, *PICK_RANGES[1], at=AT_RAW01)
-        quantize_w(1, (1,), round_w(1, (1,)))
-
-        y = [sbuf([P, S], F32, "y0")]
+        y = [sbuf([P, S], F32, "y%d" % b) for b in range(N // P)]
         for c, (lo, hi) in enumerate(CHUNKS[0]):
             product(accs[0][c][:], 0, 1, lo, hi)
-            if c in VECTOR_CHUNKS:
-                nc.vector.tensor_scalar_max(y[0][:, lo:hi], accs[0][c][:], 0.0)
-            else:
-                nc.scalar.activation(y[0][:, lo:hi], accs[0][c][:], RELU)
+            relu(nc.vector if c in VECTOR_CHUNKS else nc.scalar, 0, accs[0][c][:], lo, hi)
 
         fetch(0, 0)
         fetch_and_add(0, 0)
         accs.append(accumulators(1))
         for acc, (first, last) in zip(accs[1], CHUNKS[1]):
-            borders = [first] + [lo for lo, hi in PICK_RANGES if first < lo < last] + [last]
+            borders = [first] + [lo for lo, hi in CHUNKS[0][2:] if first < lo < last] + [last]
             for lo, hi in zip(borders, borders[1:]):
-                opening = 0 if first == 0 else 1
-                for z in (opening, 1 - opening):
-                    product(acc[:, lo - first : hi - first], 1, z, lo, hi, opening)
-        y.append(sbuf([P, S], F32, "y1", at=AT_RAW0))
+                for z in range(PASSES):
+                    product(acc[:, lo - first : hi - first], 1, z, lo, hi)
         for acc, (lo, hi) in zip(accs[1], CHUNKS[1]):
-            nc.scalar.activation(y[1][:, lo:hi], acc[:], RELU)
+            relu(nc.scalar, 1, acc[:], lo, hi)
         add(0, 0)
         fetch(0, 1)
         fetch_and_add(0, 1)

@@ -27,25 +27,26 @@ WORD_BYTES = 4
 ALIGN = 64
 MOVE_ORDER = (0, 2, 1, 3)
 
-PICK_RANGES = ((0, 512), (512, 896), (896, 1024))
+PICK_RANGES = ((0, 512), (512, 1024))
 CHUNKS = (
     ((0, 256), (256, 512), (512, 768), (768, 896), (896, 1024)),
     ((0, 512), (512, 1024)),
 )
-VECTOR_CHUNKS = (1, 3)
 BANKS = ((0, 1, 2, 3, 4), (5, 6))
+VECTOR_CHUNKS = (1, 3)
+VECTOR_COLUMNS = 88
 
 FUSED = (((0, 576), (960, 1600)), ((0, 416), (1056, 1280)))
 SHARED = (((576, 960), (1600, 2048)), ((416, 1056), (1280, 1664), (1664, 1920), (1920, 2048)))
-STORES = (((0, 960), (960, 2048)), ((0, 416), (416, 1056), (1056, 1280), (1280, 1664), (1664, 1920), (1920, 2048)))
+STORES = (((0, 960), (960, 1600), (1600, 2048)), ((0, 416), (416, 1056), (1056, 1280), (1280, 1664), (1664, 1920), (1920, 2048)))
 RES_RANGES = (((0, 576), (576, 2048)), ((0, 2048),))
 SUMS_AT = {}
 
 QUARTER = PACK * P
-LATE_WEIGHTS = 3 * QUARTER
+LATE_WEIGHTS = QUARTER
 AT_ROUNDED00 = 0
-AT_ROUNDED10 = AT_ROUNDED00 + 4 * QUARTER
-AT_SCALES = AT_ROUNDED10 + 2 * QUARTER
+AT_RAW1 = AT_ROUNDED00 + 4 * QUARTER
+AT_SCALES = AT_RAW1 + 2 * WORD_BYTES * QUARTER - ALIGN
 AT_LATE = AT_SCALES + T - ALIGN
 
 
@@ -174,16 +175,16 @@ def tile_picked_unmerge_relu_p_kernel(tc, x_words, x_scales, w1, res, offs, own,
 
         nc.sync.dma_start(scales[first_row:, :].bitcast(I32), x_scales.rearrange("z r n -> r z n").bitcast(I32))
         nc.sync.dma_start(offs_sb[:], offs)
-        nc.sync.dma_start(own_sb[:], own)
         load_words(0)
         load_words(1)
         load_w(0, (0,), sbuf([P, QUARTER], F32, "raw00")[:])
+        nc.sync.dma_start(own_sb[:], own)
 
         nc.vector.tensor_copy(picked_scales[:], scales[:].indirect(offs_sb[:]))
         place_scales()
+        load_w(1, (0, 1), sbuf([P, 2 * QUARTER], F32, "raw1", at=AT_RAW1)[:])
         late = sbuf([P, LATE_WEIGHTS + N // P * U], F32, "late", at=AT_LATE)
-        for n, (z, b) in enumerate(((1, 0), (0, 1), (1, 1))):
-            load_w(z, (b,), late[:, n * QUARTER : (n + 1) * QUARTER])
+        load_w(0, (1,), late[:, :QUARTER])
         for b in range(N // P):
             for lo, hi in RES_RANGES[b]:
                 load_res(b, lo, hi)
@@ -197,14 +198,14 @@ def tile_picked_unmerge_relu_p_kernel(tc, x_words, x_scales, w1, res, offs, own,
         for acc, (lo, hi) in zip(accs[0], CHUNKS[0]):
             product(acc[:], 0, 0, lo, hi)
         pick_words(1, *PICK_RANGES[1], at=AT_ROUNDED00)
-        rounded10 = sbuf([P, QUARTER], BF16, "rounded10", at=AT_ROUNDED10)
-        round_w(nc.scalar, 1, 0, rounded10)
+        rounded10 = sbuf([P, QUARTER], BF16, "rounded10")
+        round_w(nc.vector, 1, 0, rounded10, 0, VECTOR_COLUMNS)
+        round_w(nc.scalar, 1, 0, rounded10, VECTOR_COLUMNS, P)
         quantize_w(((1, 0),), rounded10)
-        pick_words(1, *PICK_RANGES[2], at=AT_ROUNDED10)
-        rounded_late = sbuf([P, 2 * QUARTER], BF16, "rounded_late")
-        round_w(nc.scalar, 0, 1, rounded_late[:, :QUARTER])
-        round_w(nc.scalar, 1, 1, rounded_late[:, QUARTER:])
-        quantize_w(((0, 1), (1, 1)), rounded_late)
+        for z in (1, 0):
+            rounded = sbuf([P, QUARTER], BF16, "rounded%d1" % z)
+            round_w(nc.scalar, z, 1, rounded)
+            quantize_w(((z, 1),), rounded)
 
         y = [sbuf([P, S], F32, "y%d" % b) for b in range(N // P)]
         for c, (lo, hi) in enumerate(CHUNKS[0]):
@@ -214,11 +215,9 @@ def tile_picked_unmerge_relu_p_kernel(tc, x_words, x_scales, w1, res, offs, own,
         fetch(0, 0)
         fetch_and_add(0, 0)
         accs.append(accumulators(1))
-        for acc, (first, last) in zip(accs[1], CHUNKS[1]):
-            borders = [first] + [lo for lo, hi in CHUNKS[0][2:] if first < lo < last] + [last]
-            for lo, hi in zip(borders, borders[1:]):
-                for z in range(PASSES):
-                    product(acc[:, lo - first : hi - first], 1, z, lo, hi)
+        for z in (1, 0):
+            for acc, (lo, hi) in zip(accs[1], CHUNKS[1]):
+                product(acc[:], 1, z, lo, hi, opening=1)
         for acc, (lo, hi) in zip(accs[1], CHUNKS[1]):
             relu(nc.scalar, 1, acc[:], lo, hi)
         add(0, 0)

@@ -27,14 +27,13 @@ WORD_BYTES = 4
 ALIGN = 64
 MOVE_ORDER = (0, 2, 1, 3)
 
-PICK_RANGES = ((0, 512), (512, 1024))
+PICK_RANGES = ((0, 896), (896, 1024))
 CHUNKS = (
     ((0, 256), (256, 512), (512, 768), (768, 896), (896, 1024)),
     ((0, 512), (512, 1024)),
 )
 BANKS = ((0, 1, 2, 3, 4), (5, 6))
 VECTOR_CHUNKS = (1, 3)
-VECTOR_COLUMNS = 88
 
 FUSED = (((0, 576), (960, 1600)), ((0, 416), (1056, 1280)))
 SHARED = (((576, 960), (1600, 2048)), ((416, 1056), (1280, 1664), (1664, 1920), (1920, 2048)))
@@ -45,7 +44,8 @@ SUMS_AT = {}
 QUARTER = PACK * P
 LATE_WEIGHTS = QUARTER
 AT_ROUNDED00 = 0
-AT_RAW1 = AT_ROUNDED00 + 4 * QUARTER
+AT_ROUNDED10 = AT_ROUNDED00 + WORD_BYTES * S
+AT_RAW1 = AT_ROUNDED10 + 2 * QUARTER
 AT_SCALES = AT_RAW1 + 2 * WORD_BYTES * QUARTER - ALIGN
 AT_LATE = AT_SCALES + T - ALIGN
 
@@ -126,7 +126,7 @@ def tile_picked_unmerge_relu_p_kernel(tc, x_words, x_scales, w1, res, offs, own,
         def accumulators(b):
             return [psum.tile([P, hi - lo], F32, name="acc%d_%d" % (b, lo), tag="bank%d" % BANKS[b][c]) for c, (lo, hi) in enumerate(CHUNKS[b])]
 
-        def product(acc, b, z, lo, hi, opening=0):
+        def product(acc, b, z, lo, hi, opening=0, opens=True):
             first = max(start for pass_of_tile, start in picked_words if pass_of_tile == z and start <= lo)
             nc.tensor.matmul_mx(
                 out=acc,
@@ -134,7 +134,7 @@ def tile_picked_unmerge_relu_p_kernel(tc, x_words, x_scales, w1, res, offs, own,
                 lhsT_scale=w_scales[z, b],
                 rhs=picked_words[z, first][:, lo - first : hi - first].bitcast(FP8X4),
                 rhs_scale=placed_scales[:, z * S + lo : z * S + hi],
-                start=(z == opening),
+                start=(z == opening and opens),
                 stop=(z != opening),
             )
 
@@ -176,8 +176,8 @@ def tile_picked_unmerge_relu_p_kernel(tc, x_words, x_scales, w1, res, offs, own,
         nc.sync.dma_start(scales[first_row:, :].bitcast(I32), x_scales.rearrange("z r n -> r z n").bitcast(I32))
         nc.sync.dma_start(offs_sb[:], offs)
         load_words(0)
-        load_words(1)
         load_w(0, (0,), sbuf([P, QUARTER], F32, "raw00")[:])
+        load_words(1)
         nc.sync.dma_start(own_sb[:], own)
 
         nc.vector.tensor_copy(picked_scales[:], scales[:].indirect(offs_sb[:]))
@@ -190,18 +190,17 @@ def tile_picked_unmerge_relu_p_kernel(tc, x_words, x_scales, w1, res, offs, own,
                 load_res(b, lo, hi)
 
         pick_words(0, 0, S)
-        pick_words(1, *PICK_RANGES[0])
         rounded00 = sbuf([P, QUARTER], BF16, "rounded00", at=AT_ROUNDED00)
         round_w(nc.scalar, 0, 0, rounded00)
         quantize_w(((0, 0),), rounded00)
         accs = [accumulators(0)]
         for acc, (lo, hi) in zip(accs[0], CHUNKS[0]):
             product(acc[:], 0, 0, lo, hi)
-        pick_words(1, *PICK_RANGES[1], at=AT_ROUNDED00)
-        rounded10 = sbuf([P, QUARTER], BF16, "rounded10")
-        round_w(nc.vector, 1, 0, rounded10, 0, VECTOR_COLUMNS)
-        round_w(nc.scalar, 1, 0, rounded10, VECTOR_COLUMNS, P)
+        pick_words(1, *PICK_RANGES[0], at=AT_ROUNDED00)
+        rounded10 = sbuf([P, QUARTER], BF16, "rounded10", at=AT_ROUNDED10)
+        round_w(nc.scalar, 1, 0, rounded10)
         quantize_w(((1, 0),), rounded10)
+        pick_words(1, *PICK_RANGES[1], at=AT_ROUNDED10)
         for z in (1, 0):
             rounded = sbuf([P, QUARTER], BF16, "rounded%d1" % z)
             round_w(nc.scalar, z, 1, rounded)
@@ -215,9 +214,11 @@ def tile_picked_unmerge_relu_p_kernel(tc, x_words, x_scales, w1, res, offs, own,
         fetch(0, 0)
         fetch_and_add(0, 0)
         accs.append(accumulators(1))
-        for z in (1, 0):
-            for acc, (lo, hi) in zip(accs[1], CHUNKS[1]):
-                product(acc[:], 1, z, lo, hi, opening=1)
+        for z, cuts in ((1, CHUNKS[1][:1] + CHUNKS[0][2:]), (0, CHUNKS[1])):
+            for lo, hi in cuts:
+                c = lo // CHUNKS[1][1][0]
+                first = CHUNKS[1][c][0]
+                product(accs[1][c][:, lo - first : hi - first], 1, z, lo, hi, opening=1, opens=(lo == first))
         for acc, (lo, hi) in zip(accs[1], CHUNKS[1]):
             relu(nc.scalar, 1, acc[:], lo, hi)
         add(0, 0)

from contextlib import ExitStack

import concourse.mybir as mybir

K, T, S, N, U = 1024, 2048, 1024, 256, 2048
FLOPS = 2 * K * N * S

F32 = mybir.dt.float32
BF16 = mybir.dt.bfloat16
I32 = mybir.dt.int32
U32 = mybir.dt.uint32
U16 = mybir.dt.uint16
U8 = mybir.dt.uint8
FP8X4 = mybir.dt.float8_e4m3fn_x4
RELU = mybir.ActivationFunctionType.Relu
COPY = mybir.ActivationFunctionType.Copy
ADD = mybir.AluOpType.add

P = 128
PACK = 4
PASSES = K // (P * PACK)
QUADRANT = 32
SCALE_ROWS = K // 32
ENTRIES_PER_COLUMN = 16
LINE = 4
WORD_BYTES = 4
ALIGN = 64
MOVE_ORDER = (0, 2, 1, 3)

PICK_RANGES = ((0, 896), (896, 1024))
CHUNKS = (
    ((0, 256), (256, 512), (512, 768), (768, 896), (896, 1024)),
    ((0, 512), (512, 1024)),
)
BANKS = ((0, 1, 2, 3, 4), (5, 6))
VECTOR_CHUNKS = (1, 3)

FUSED = (((0, 576), (960, 1600)), ((0, 416), (1056, 1280)))
SHARED = (((576, 960), (1600, 2048)), ((416, 1056), (1280, 1664), (1664, 1920), (1920, 2048)))
STORES = (((0, 960), (960, 1600), (1600, 2048)), ((0, 416), (416, 1056), (1056, 1280), (1280, 1664), (1664, 1920), (1920, 2048)))
RES_RANGES = (((0, 576), (576, 2048)), ((0, 2048),))
SUMS_AT = {}

QUARTER = PACK * P
LATE_WEIGHTS = QUARTER
AT_ROUNDED00 = 0
AT_ROUNDED10 = AT_ROUNDED00 + WORD_BYTES * S
AT_RAW1 = AT_ROUNDED10 + 2 * QUARTER
AT_SCALES = AT_RAW1 + 2 * WORD_BYTES * QUARTER - ALIGN
AT_LATE = AT_SCALES + T - ALIGN


def tile_picked_unmerge_relu_p_kernel(tc, x_words, x_scales, w1, res, offs, own, out):
    nc = tc.nc
    with ExitStack() as ctx:
        keep = ctx.enter_context(tc.tile_pool(name="keep", bufs=1))
        laid = ctx.enter_context(tc.tile_pool(name="laid", bufs=1))
        psum = ctx.enter_context(tc.psum_pool(name="psum", bufs=1))

        def sbuf(shape, dtype, name, at=None):
            if at is not None:
                return laid.tile(shape, dtype, name=name, tag=name, align_bytes=ALIGN, offset=at)
            return keep.tile(shape, dtype, name=name, tag=name, align_bytes=ALIGN)

        def entries(list_tile, lo, hi):
            return list_tile[:, lo // ENTRIES_PER_COLUMN : hi // ENTRIES_PER_COLUMN]

        offs_sb = keep.tile([P, S // ENTRIES_PER_COLUMN], U16, name="offs_sb")
        own_sb = keep.tile([P, U // ENTRIES_PER_COLUMN], U16, name="own_sb")
        words = [sbuf([P, T], I32, "words%d" % z) for z in range(PASSES)]
        scales = sbuf([P, T], U8, "scales", at=AT_SCALES)
        picked_scales = sbuf([P, S], U8, "picked_scales")
        placed_scales = sbuf([P, PASSES * S], U8, "placed_scales")
        w_raw, w_codes, w_scales = {}, {}, {}
        picked_words = {}
        sums = {}
        first_row = P - SCALE_ROWS

        def load_words(z):
            nc.sync.dma_start(words[z][:], x_words[z].rearrange("p n t -> p (n t)").bitcast(I32))

        def load_w(z, blocks, tile):
            whole = tile.rearrange("p (t m) -> p t m", t=PACK)
            for n, b in enumerate(blocks):
                w_raw[z, b] = whole[:, :, n * P : (n + 1) * P]
            rows = w1[z * P * PACK : (z + 1) * P * PACK, blocks[0] * P : (blocks[-1] + 1) * P]
            nc.sync.dma_start(whole, rows.rearrange("(p t) m -> p t m", t=PACK))

        def res_columns(b, lo, hi):
            first = LATE_WEIGHTS + b * U
            return late[:, first + lo : first + hi]

        def load_res(b, lo, hi):
            nc.sync.dma_start(res_columns(b, lo, hi), res[b * P : (b + 1) * P, lo:hi])

        def place_scales():
            rows = PACK * PASSES
            for q in MOVE_ORDER:
                row = first_row + rows * q
                nc.sync.dma_start(
                    placed_scales[QUADRANT * q : QUADRANT * q + PACK, :].bitcast(I32),
                    picked_scales[row : row + rows, :].bitcast(I32),
                )

        def round_w(engine, z, b, rounded, lo=0, hi=P):
            target = rounded[:, PACK * lo : PACK * hi].rearrange("p (c i t) -> p c t i", i=LINE, t=PACK)
            source = w_raw[z, b][:, :, lo:hi].rearrange("p t (c i) -> p c t i", i=LINE)
            if engine is nc.scalar:
                nc.scalar.activation(target, source, COPY)
            else:
                engine.tensor_copy(target, source)

        def quantize_w(quarters, rounded):
            name = "".join(["%d%d" % quarter for quarter in quarters])
            codes = sbuf([P, P * len(quarters)], U32, "w_codes" + name)
            planes = sbuf([P, P * len(quarters)], U8, "w_scales" + name)
            nc.vector.quantize_mx(out=codes[:].bitcast(FP8X4), scales=planes[:], in_=rounded[:])
            for n, quarter in enumerate(quarters):
                w_codes[quarter] = codes[:, n * P : (n + 1) * P]
                w_scales[quarter] = planes[:, n * P : (n + 1) * P]

        def pick_words(z, lo, hi, at=None):
            picked_words[z, lo] = sbuf([P, hi - lo], U32, "picked_words%d_%d" % (z, lo), at)
            nc.vector.tensor_copy(picked_words[z, lo][:], words[z][:].bitcast(U32).indirect(entries(offs_sb, lo, hi)))

        def accumulators(b):
            return [psum.tile([P, hi - lo], F32, name="acc%d_%d" % (b, lo), tag="bank%d" % BANKS[b][c]) for c, (lo, hi) in enumerate(CHUNKS[b])]

        def product(acc, b, z, lo, hi, opening=0, opens=True):
            first = max(start for pass_of_tile, start in picked_words if pass_of_tile == z and start <= lo)
            nc.tensor.matmul_mx(
                out=acc,
                lhsT=w_codes[z, b].bitcast(FP8X4),
                lhsT_scale=w_scales[z, b],
                rhs=picked_words[z, first][:, lo - first : hi - first].bitcast(FP8X4),
                rhs_scale=placed_scales[:, z * S + lo : z * S + hi],
                start=(z == opening and opens),
                stop=(z != opening),
            )

        def relu(engine, b, acc, lo, hi):
            if engine is nc.scalar:
                nc.scalar.activation(y[b][:, lo:hi], acc, RELU)
            else:
                nc.vector.tensor_scalar_max(y[b][:, lo:hi], acc, 0.0)

        def sums_columns(b, lo, hi):
            first, last = [(start, stop) for start, stop in STORES[b] if start <= lo < stop][0]
            if (b, first) not in sums:
                sums[b, first] = sbuf([P, last - first], F32, "sums%d_%d" % (b, first), SUMS_AT.get((b, first)))
            return sums[b, first][:, lo - first : hi - first]

        def store_if_whole(b, hi):
            for first, last in STORES[b]:
                if last == hi:
                    nc.sync.dma_start(out[b * P : (b + 1) * P, first:last], sums[b, first][:])

        def fetch_and_add(b, n):
            lo, hi = FUSED[b][n]
            picked_y = y[b][:].indirect(entries(own_sb, lo, hi))
            nc.vector.tensor_tensor(sums_columns(b, lo, hi), picked_y, res_columns(b, lo, hi), ADD)
            store_if_whole(b, hi)

        def fetch(b, n):
            lo, hi = SHARED[b][n]
            nc.scalar.activation(sums_columns(b, lo, hi), y[b][:].indirect(entries(own_sb, lo, hi)), COPY)

        def add(b, n):
            lo, hi = SHARED[b][n]
            nc.vector.tensor_tensor(sums_columns(b, lo, hi), sums_columns(b, lo, hi), res_columns(b, lo, hi), ADD)
            store_if_whole(b, hi)

        nc.vector.memset(scales[:first_row, :].bitcast(I32), 0)
        nc.vector.memset(placed_scales[:].bitcast(I32), 0)

        nc.sync.dma_start(scales[first_row:, :].bitcast(I32), x_scales.rearrange("z r n -> r z n").bitcast(I32))
        nc.sync.dma_start(offs_sb[:], offs)
        load_words(0)
        load_w(0, (0,), sbuf([P, QUARTER], F32, "raw00")[:])
        load_words(1)
        nc.sync.dma_start(own_sb[:], own)

        nc.vector.tensor_copy(picked_scales[:], scales[:].indirect(offs_sb[:]))
        place_scales()
        load_w(1, (0, 1), sbuf([P, 2 * QUARTER], F32, "raw1", at=AT_RAW1)[:])
        late = sbuf([P, LATE_WEIGHTS + N // P * U], F32, "late", at=AT_LATE)
        load_w(0, (1,), late[:, :QUARTER])
        for b in range(N // P):
            for lo, hi in RES_RANGES[b]:
                load_res(b, lo, hi)

        pick_words(0, 0, S)
        rounded00 = sbuf([P, QUARTER], BF16, "rounded00", at=AT_ROUNDED00)
        round_w(nc.scalar, 0, 0, rounded00)
        quantize_w(((0, 0),), rounded00)
        accs = [accumulators(0)]
        for acc, (lo, hi) in zip(accs[0], CHUNKS[0]):
            product(acc[:], 0, 0, lo, hi)
        pick_words(1, *PICK_RANGES[0], at=AT_ROUNDED00)
        rounded10 = sbuf([P, QUARTER], BF16, "rounded10", at=AT_ROUNDED10)
        round_w(nc.scalar, 1, 0, rounded10)
        quantize_w(((1, 0),), rounded10)
        pick_words(1, *PICK_RANGES[1], at=AT_ROUNDED10)
        for z in (1, 0):
            rounded = sbuf([P, QUARTER], BF16, "rounded%d1" % z)
            round_w(nc.scalar, z, 1, rounded)
            quantize_w(((z, 1),), rounded)

        y = [sbuf([P, S], F32, "y%d" % b) for b in range(N // P)]
        for c, (lo, hi) in enumerate(CHUNKS[0]):
            product(accs[0][c][:], 0, 1, lo, hi)
            relu(nc.vector if c in VECTOR_CHUNKS else nc.scalar, 0, accs[0][c][:], lo, hi)

        fetch(0, 0)
        fetch_and_add(0, 0)
        accs.append(accumulators(1))
        for z, cuts in ((1, CHUNKS[1][:1] + CHUNKS[0][2:]), (0, CHUNKS[1])):
            for lo, hi in cuts:
                c = lo // CHUNKS[1][1][0]
                first = CHUNKS[1][c][0]
                product(accs[1][c][:, lo - first : hi - first], 1, z, lo, hi, opening=1, opens=(lo == first))
        for acc, (lo, hi) in zip(accs[1], CHUNKS[1]):
            relu(nc.scalar, 1, acc[:], lo, hi)
        add(0, 0)
        fetch(0, 1)
        fetch_and_add(0, 1)
        fetch(1, 0)
        add(0, 1)
        fetch_and_add(1, 0)
        fetch(1, 1)
        add(1, 0)
        fetch_and_add(1, 1)
        fetch(1, 2)
        add(1, 1)
        fetch(1, 3)
        add(1, 2)
        add(1, 3)
